import numpy as np, ml_dtypes
CORES = [23,119,17,113]
N = 4
BF = ml_dtypes.bfloat16
def gentries(a):
    return np.ascontiguousarray(a.reshape(8, 16, -1).transpose(0, 2, 1)).reshape(8, -1)
def gtable(e):
    e = np.asarray(e); return np.ascontiguousarray(e.reshape(8, -1, 16).transpose(0, 2, 1)).reshape(128, -1).astype(np.int32)
M, L, T, H, A, R = 1792, 256, 3, 4096, 12, 1024
W = M + L * T; NONE = 4095
def hashes(w, a):
    u = np.matmul(w.transpose(0, 2, 1), a) & 4095
    return (((u[:, 0] * u[:, 1]) >> 5) + u[:, 1]) & (H - 1)
def some(rng, n, tops):
    return (rng.random((N, 8, 16, n)) * rng.choice(np.array(tops), (N, 8, 1, n))).astype(np.int64)
def places(rng, sizes):
    v = np.zeros((N, 8, L), np.int64)
    for r in range(N):
        for g in range(8):
            pool = rng.permutation(M)[:int(sizes[r, g])]; v[r, g] = pool[rng.integers(0, len(pool), L)]
    return v
def flat(a):
    return np.ascontiguousarray(a.reshape(N, 128, -1)).astype(np.float32).astype(BF)
def pack(X, B, E, x, v, w):
    return {"nodes": flat(X), "book": flat(B), "kids": np.ascontiguousarray(E.reshape(N, 128, M)).astype(np.int32), "cand": flat(x),
            "spot": np.stack([gtable(a) for a in v]), "wts": flat(w)}
def setup_inputs(rng):
    X = some(rng, M, (48, 96, 160, 256)); B = some(rng, H, (96, 160, 256)); x = some(rng, L, (96, 192, 256))
    k = np.minimum(rng.integers(0, 17, (N, 8, 16, M)), rng.integers(0, 17, (N, 8, 16, M)))
    fill = rng.choice(np.array([0.3, 0.6, 0.9, 1.0]), (N, 8, 1, M))
    E = 4096 * k + np.where(rng.random((N, 8, 16, M)) < fill, rng.integers(0, M, (N, 8, 16, M)), NONE)
    v = places(rng, rng.choice(np.array([8, 32, 128, M]), (N, 8)))
    return pack(X, B, E, x, v, rng.integers(0, 16, (N, 8, 16, 2)))
def setup_inputs_spread(rng):
    X = (np.exp2(8 * rng.random((N, 8, 1, M))) * rng.random((N, 8, 16, M))).astype(np.int64)
    x = (np.exp2(8 * rng.random((N, 8, 1, L))) * rng.random((N, 8, 16, L))).astype(np.int64); B = rng.integers(0, 256, (N, 8, 16, H))
    E = 4096 * rng.integers(0, 17, (N, 8, 16, M)) + np.where(rng.random((N, 8, 16, M)) < rng.random((N, 8, 1, M)), rng.integers(0, M, (N, 8, 16, M)), NONE)
    v = np.minimum((M * rng.random((N, 8, L)) ** 3).astype(np.int64), M - 1); w = np.minimum((16 * rng.random((N, 8, 16, 2)) ** 2).astype(np.int64), 15)
    return pack(X, B, E, x, v, w)
def setup_inputs_ends(rng):
    X = 255 * rng.integers(0, 2, (N, 8, 16, M)); B = 255 * rng.integers(0, 2, (N, 8, 16, H)); x = 255 * rng.integers(0, 2, (N, 8, 16, L))
    a = rng.random((N, 8, 1, L)); x = np.where(a < 0.15, 0, np.where(a < 0.4, 255, x))
    X[..., 0] = 0; X[..., M - 1] = 255
    w = 15 * rng.integers(0, 2, (N, 8, 16, 2)); w[:, ::2, 13] = 15; w[:, ::2, 14] = 1; w[:, ::2, 15] = 15; w[:, 7] = 15
    E = 69631 * rng.integers(0, 2, (N, 8, 16, M)); o = rng.random(E.shape)
    E = np.where(o < 0.35, rng.choice(np.array([65536, M - 1, M - 1 + 65536]), E.shape), E)
    E = np.where(o < 0.1, rng.integers(1, M - 16, E.shape) + 65536 * rng.integers(0, 2, E.shape), E)
    E[..., M - 1] = 69631 * rng.integers(0, 2, (N, 8, 16)); E[:, :, 15, M - 1] = M - 1 + 65536; low = rng.integers(0, 8, (N, 8))
    E[:, :, :15, M - 2] = 0; E[:, :, 15, M - 2] = 69631
    for j in range(1, T): E[:, :, :, M - 2 - j] = 65536 + M - 1 - j
    E[:, :, :15, M - 2 - T] = 69631; E[:, :, 15, M - 2 - T] = 0
    v = np.where(rng.random((N, 8, L)) < 0.68, (M - 1) * rng.integers(0, 2, (N, 8, L)), rng.integers(1, M - 16, (N, 8, L)))
    v[:, :, L - 1] = M - 1 - T; x[..., L - 1] = 255
    v[:, :, L - 17] = M - 1; x[..., L - 17] = 255
    v[:, :, L - 33] = M - 2 - T; x[..., L - 33] = 255
    v[:, :, L - 2] = M - 1; x[:, ::2, :, L - 2] = 0; x[:, ::2, 14:, L - 2] = 255; x[:, ::2, 13, L - 2] = 1
    s = rng.integers(0, 2, (N, 8)); s[:, 7] = 1; s[:, 1] = 0
    for r in range(N):
        h = hashes(w[r], np.full((8, 16, 1), 255))[:, 0]
        for g in range(8):
            B[r, g, :, h[g]] = 255 * s[r, g]; E[r, g, low[r, g], M - 1] = 65536
    return pack(X, B, E, x, v, w)
def setup_inputs_corners(rng):
    X = some(rng, M, (2, 64, 256)); B = some(rng, H, (2, 128, 256))
    kind = rng.integers(0, 9, (N, 8, 1, M)); kind[..., 5:6 + T] = 4
    own = np.arange(M); one = rng.integers(0, 16, (N, 8, 1, M)); line = np.arange(16)[:, None]
    c = rng.integers(0, M, (N, 8, 16, M))
    c = np.where(kind == 3, own, np.where(kind == 4, (own + 1) % M, np.where(kind == 5, 0, np.where(kind == 6, M - 1, c))))
    hide = (kind == 0) | ((kind == 2) & (line != one)) | ((kind == 7) & (line == one)) | ((kind == 8) & (rng.random(c.shape) < 0.5))
    m = rng.integers(0, 4, (N, 8, 1, M)); m = np.where(kind == 4, 1, m)
    k = np.where(m == 0, 0, np.where(m == 1, 16, np.where(m == 2, 15, rng.integers(0, 17, c.shape))))
    E = 4096 * k + np.where(hide, NONE, c)
    v = rng.integers(0, M, (N, 8, L)); w = rng.integers(0, 16, (N, 8, 16, 2))
    for r in range(N):
        o = rng.permutation(8); q = rng.permutation(M)
        v[r, o[0]] = 0; v[r, o[1]] = M - 1; v[r, o[2]] = q[:L]; v[r, o[3]] = rng.permutation(np.repeat(q[:L // 2], 2))
        v[r, o[4]] = rng.choice(np.array([5, 0, M - 1, 6]), L); v[r, o[5], ::2] = 5; v[r, o[5], L - 1] = 5
        b = rng.permutation(8)
        w[r, b[0]] = 0; w[r, b[1]] = 15; w[r, b[2], 1:] = 0; w[r, b[2], 0] = 15; w[r, b[3], :15] = 0; w[r, b[3], 15] = 15; w[r, b[4], :, 0] = 0; w[r, b[5], :, 1] = 0
    d = rng.integers(0, 4, (N, 8, 1, L)); x = some(rng, L, (64, 256))
    x = np.where(d == 0, 0, np.where(d == 1, 255, np.where(d == 2, np.take_along_axis(X, v[:, :, None, :], 3), x)))
    return pack(X, B, E, x, v, w)
def full(rng, X, B, E, x, v, r, late):
    n = T - 1 if late else 0; half = rng.permutation(8)
    for g in range(8):
        u = rng.permutation(M)[:L * T].reshape(T, L); e = E[r, g]; v[r, g] = u[0]
        for j in range(n): e[:, u[j]] = 65536 + u[j + 1][None, :]
        if half[g] < 4:
            e[:, u[n]] = NONE + 4096 * rng.integers(0, 17, (16, L))
        else:
            X[r, g] = rng.integers(0, 8, (16, M)); x[r, g] = rng.integers(8, 24, (16, L)); B[r, g] = rng.integers(24, 256, (16, H))
            e[:, u[n]] = rng.integers(0, M, (16, L)) + 4096 * rng.integers(0, 16, (16, L))
def setup_inputs_crowd(rng):
    X = some(rng, M, (16, 64, 128)); B = some(rng, H, (160, 256)); x = np.minimum(some(rng, L, (128, 256)) + rng.integers(0, 64, (N, 8, 1, L)), 255)
    k = rng.integers(0, 17, (N, 8, 16, M)) * (rng.random((N, 8, 16, M)) < 0.3); fill = rng.choice(np.array([0.5, 1.0]), (N, 8, 1, M))
    E = 4096 * k + np.where(rng.random((N, 8, 16, M)) < fill, rng.integers(0, M, (N, 8, 16, M)), NONE)
    v = places(rng, rng.choice(np.array([1, 2, 3, 16]), (N, 8))); v[:, 0] = 0; v[:, 7] = M - 1
    o = rng.permutation(N); full(rng, X, B, E, x, v, int(o[0]), False); full(rng, X, B, E, x, v, int(o[1]), True)
    return pack(X, B, E, x, v, rng.integers(0, 16, (N, 8, 16, 2)))
def setup_inputs_ties(rng):
    X = 100 + rng.integers(0, 3, (N, 8, 16, M)); x = 100 + rng.integers(0, 3, (N, 8, 16, L)); B = rng.integers(0, 3, (N, 8, 16, H))
    c = rng.integers(0, M, (N, 8, 16, M)); c[:, ::2, 8:] = c[:, ::2, :8]
    E = 4096 * rng.integers(8, 15, c.shape) + np.where(rng.random(c.shape) < 0.8, c, NONE)
    v = places(rng, rng.choice(np.array([4, 16, 64, M]), (N, 8)))
    return pack(X, B, E, x, v, rng.integers(0, 16, (N, 8, 16, 2)))
def check_inputs(d):
    bad = []
    for k, lo, hi in (("nodes", 0, 255), ("book", 0, 255), ("kids", 0, 69631), ("cand", 0, 255), ("spot", 0, M - 1), ("wts", 0, 15)):
        a = np.asarray(d[k]).astype(np.float32)
        if not (np.min(a) >= lo and np.max(a) <= hi and np.all(a == np.floor(a))): bad.append("range of " + k)
    c = np.asarray(d["kids"]).astype(np.int64) & 4095
    if np.any((c >= M) & (c != NONE)): bad.append("children in kids")
    return bad
def reference(nodes, book, kids, cand, spot, wts):
    X = np.zeros((N, 8, 16, W), np.int64); X[..., :M] = nodes.astype(np.float32).astype(np.int64).reshape(N, 8, 16, M)
    E = np.full((N, 8, 16, W), NONE, np.int64); E[..., :M] = kids.astype(np.int64).reshape(N, 8, 16, M)
    B = book.astype(np.float32).astype(np.int64).reshape(N, 8, 16, H); w = wts.astype(np.float32).astype(np.int64).reshape(N, 8, 16, 2)
    xs = cand.astype(np.float32).astype(np.int64).reshape(N, 8, 16, L).copy(); vs = np.stack([gentries(a) for a in spot]).astype(np.int64)
    lane = np.arange(L); p = lane & 15; gr = np.arange(8)[:, None]
    for t in range(T):
        for r in range(N):
            x, v, q = xs[r], vs[r], (r + 1 + t % (N - 1)) % N
            ev = np.take_along_axis(E[r], v[:, None, :], 2)
            c = ev & 4095; thr = ev >> 12; filled = c != NONE
            xc = np.take_along_axis(X[r], np.where(filled, c, 0).reshape(8, 1, 16 * L), 2).reshape(8, 16, 16, L)
            dif = np.abs(x[:, :, None, :] - xc); fd = dif.reshape(8, 16, 16 * L)
            bc = np.take_along_axis(B[r], hashes(w[r], fd)[:, None, :], 2)
            s = np.add.reduce((bc >= fd).astype(np.int64), axis=1).reshape(8, 16, L)
            over = np.add.reduce((x[:, :, None, :] >= xc).astype(np.int64), axis=1)
            cap = filled & (over >= A) & (s > thr); stay = filled & ~cap
            go = stay[:, p, lane]
            best = np.argmax(np.where(stay, s, -1), axis=1)
            down = np.take_along_axis(c, best[:, None, :], 1)[:, 0]
            first = np.full((8, W), L); np.minimum.at(first, (gr, v), np.where(go, L, lane[None, :]))
            win = ~go & (first[gr, v] == lane[None, :]); wb = win[:, None, :]
            z = np.abs(np.take_along_axis(X[r], v[:, None, :], 2) - x)
            y = np.take_along_axis(B[q], hashes(w[q], z)[:, None, :], 2)
            n = M + L * t + lane
            X[r][:, :, M + L * t:M + L * t + L] = np.where(wb, x, 0)
            E[r][:, :, M + L * t:M + L * t + L] = np.where(wb & cap, c + 4096 * s, NONE)
            col = np.where(cap, NONE, ev); col[:, p, lane] = n[None, :] + 4096 * np.max(np.where(cap, s, 0), axis=1)
            gi, li = np.nonzero(win)
            E[r][gi, :, v[gi, li]] = col[gi, :, li]
            x = np.where(wb, np.abs(x - y), x)
            back = np.add.reduce(w[r][:, :, 0:1] * x, axis=1) & (R - 1)
            xs[r] = x; vs[r] = np.where(win, back, np.where(go, down, v))
    return {"ykids": E.reshape(N, 128, W).astype(np.float32), "ynodes": np.ascontiguousarray(X[..., M:]).reshape(N, 128, L * T).astype(np.float32).astype(BF),
            "ycand": xs.reshape(N, 128, L).astype(np.float32).astype(BF), "yspot": np.stack([gtable(a) for a in vs]).astype(np.float32)}

@@ -1,0 +1,485 @@
+from concourse.mybir import dt, AluOpType as A, ActivationFunctionType as F
+
+M, L, STEPS, H = 1792, 256, 3, 4096
+W = M + L * STEPS
+NENG = 8
+BIG = float(2 ** 23)
+
+SB = {
+    "XT": (4096, "bfloat16"), "BK": (4096, "bfloat16"), "ET": (2944, "float32"), "KI": (M, "int32"), "IDX": (2304, "float32"),
+    "ONE": (1024, "bfloat16"), "ZER": (128, "bfloat16"), "IDb": (128, "bfloat16"), "NIDb": (128, "bfloat16"), "IDf": (128, "float32"), "NIDf": (128, "float32"),
+    "N20": (128, "bfloat16"), "N22": (128, "bfloat16"), "I4K": (128, "bfloat16"), "G8t": (8, "bfloat16"), "G8": (8, "bfloat16"), "G8f": (8, "float32"),
+    "GW": (16, "float32"), "W1": (2048, "bfloat16"), "W2": (2048, "bfloat16"), "GS": (24, "bfloat16"), "GO": (8, "bfloat16"),
+    "PICK": (1024, "bfloat16"), "PK8": (8, "bfloat16"), "TRI": (128, "bfloat16"), "pms": (128, "bfloat16"), "pm": (256, "bfloat16"), "npm": (256, "bfloat16"),
+    "pmn": (256, "float32"), "rmf": (128, "float32"), "rmb": (128, "bfloat16"), "CR": (512, "bfloat16"), "REP": (2048, "bfloat16"), "trash": (16, "float32"),
+    "II": (256, "float32"), "CA0": (256, "float32"), "CA1": (256, "float32"), "pm256": (256, "float32"),
+    "wt": (2, "bfloat16"), "sp": (16, "int32"), "x0": (256, "bfloat16"), "x1": (256, "bfloat16"), "lv0": (16, "float32"), "lv1": (16, "float32"), "lvu": (16, "uint16"),
+    "Ei": (256, "int32"), "Ci": (256, "int32"), "CL": (256, "uint16"), "Ff": (256, "float32"), "em": (256, "bfloat16"), "Cm": (256, "float16"), "Rm": (256, "float32"),
+    "vA": (256, "float16"), "vcol": (16, "float32"), "xT": (256, "bfloat16"), "d0": (256, "bfloat16"),
+    "XG": (4096, "bfloat16"), "DD": (4096, "bfloat16"), "SG": (4096, "bfloat16"), "CMP": (4096, "bfloat16"), "HL": (256, "uint16"),
+    "hu": (128, "int32"), "hp": (64, "int32"), "ru": (32, "int32"), "rp": (16, "int32"), "rl": (16, "uint16"), "MQ": (3072, "bfloat16"),
+    "tA": (256, "float32"), "cap": (256, "bfloat16"), "nc": (256, "bfloat16"), "key": (256, "float32"), "wm": (256, "bfloat16"), "w1s": (256, "bfloat16"), "wb": (256, "bfloat16"),
+    "k1": (256, "float32"), "k2": (256, "float32"), "dpm": (256, "float32"), "NE": (256, "float32"), "n1": (256, "float32"), "n2": (256, "float32"), "Si": (256, "int32"), "pS": (256, "bfloat16"),
+    "r2": (256, "float32"), "winb": (256, "bfloat16"), "winm": (256, "bfloat16"), "newc": (256, "float32"), "NEs": (256, "float32"), "NEw": (256, "float32"),
+    "rr": (256, "bfloat16"), "rx": (256, "bfloat16"), "ws": (32, "float32"), "of": (16, "float32"), "ofu": (16, "uint16"), "vt": (16, "float32"),
+    "dn": (16, "int32"), "b1": (16, "float32"), "b2": (16, "float32"), "bi": (16, "int32"), "bk": (16, "int32"),
+}
+for _t in range(STEPS):
+    for _n in ("z", "zl", "yr", "yl"):
+        SB[_n + str(_t)] = (256, "bfloat16")
+PS = ["dp0", "dp1", "up", "BH0", "BH1", "ov", "m0", "m1"]
+SCRATCH = {k: ("sbuf", [128, n], d) for k, (n, d) in SB.items()}
+for _n in PS:
+    SCRATCH[_n] = ("psum", [128, 512], "float32")
+NDMA = 10
+SEMAPHORES = ["qv", "qs", "qt", "qg"] + ["D%d" % i for i in range(NDMA)] + [n + str(t) for t in range(STEPS) for n in ("zs", "za", "ys", "ya")]
+
+
+def rank_program(g, core, T, topo):
+    rank = T.rank_of(core)
+    if rank is None:
+        return
+    queues = {"v": g.vector, "s": g.scalar, "t": g.tensor, "g": g, "y": g.sync}
+    known = {q: {} for q in queues}
+    count = {}
+    clock = {}
+    hist = {}
+
+    def R(name, lo=0, hi=None, step=1, p1=128):
+        return (name, lo, SB[name][0] if hi is None and name in SB else (512 if hi is None else hi), step, p1)
+
+    def P(name, win, off):
+        return ("ind", win, off)
+
+    def ap(r):
+        if r[0] == "ind":
+            return ap(r[1]).indirect(ap(r[2]))
+        name, lo, hi, step, p1 = r
+        if step == -1:
+            return T[name][:, hi - 1:(lo - 1 if lo > 0 else None):-1]
+        if p1 != 128:
+            return T[name][0:p1, lo:hi]
+        return T[name][:, lo:hi] if step == 1 else T[name][:, lo:hi:step]
+
+    def flat(rs):
+        out = []
+        for r in rs:
+            out += [r[1], r[2]] if r[0] == "ind" else [r]
+        return out
+
+    def need(q, ev):
+        sem, val = ev
+        k = known[q]
+        if k.get(sem, 0) >= val:
+            return
+        queues[q].wait_ge(T.sem[sem], val)
+        k[sem] = val
+        for s2, v2 in clock.get(ev, {}).items():
+            if k.get(s2, 0) < v2:
+                k[s2] = v2
+
+    def deps(q, me, reads, writes):
+        evs = {}
+        for rs, w in ((reads, False), (writes, True)):
+            for r in rs:
+                bank = r[0] in PS
+                for (who, ev, lo, hi, wasw, step) in hist.get(r[0], ()):
+                    over = lo < r[2] and r[1] < hi and not (step == r[3] and step > 1 and (lo - r[1]) % step)
+                    if who == me:
+                        if not wasw or not over or (w and me == "t"):
+                            continue
+                    elif not (bank or (over and (w or wasw))):
+                        continue
+                    if evs.get(ev[0], 0) < ev[1]:
+                        evs[ev[0]] = ev[1]
+        for sem in sorted(evs):
+            need(q, (sem, evs[sem]))
+
+    def note(me, ev, reads, writes):
+        for rs, w in ((reads, False), (writes, True)):
+            for r in rs:
+                old = hist.get(r[0], [])
+                if w and abs(r[3]) == 1 and r[4] == 128:
+                    old = [e for e in old if not (r[1] <= e[2] and e[3] <= r[2])]
+                else:
+                    old = [e for e in old if not (e[0] == me and e[2:] == (r[1], r[2], w, abs(r[3])))]
+                hist[r[0]] = old + [(me, ev, r[1], r[2], w, abs(r[3]))]
+
+    def emit(q, fn, reads, writes):
+        reads, writes = flat(reads), flat(writes)
+        deps(q, q, reads, writes)
+        ins = fn()
+        sem = "q" + q
+        count[sem] = count.get(sem, 0) + 1
+        ins.then_inc(T.sem[sem], 1)
+        ev = (sem, count[sem])
+        clock[ev] = dict(known[q])
+        note(q, ev, reads, writes)
+
+    nd = [0]
+
+    def dma(q, out, in_, reads, writes):
+        sem = "D%d" % nd[0]
+        nd[0] += 1
+        deps(q, sem, reads, writes)
+        queues[q].dma_start(out, in_).then_inc(T.sem[sem], 16)
+        count[sem] = 16
+        clock[(sem, 16)] = dict(known[q])
+        note(sem, (sem, 16), reads, writes)
+
+    def send(src, dst, peer, lsem, rsem):
+        to = T.cores[peer]
+        rid, pid = topo.addr(to)[:2]
+        engs = topo.engines(core, to)[:NENG]
+        deps("g", lsem, [R(src)], [])
+        g.remote_dma(T[dst][:], T[src][:], T.sem[rsem], T.sem[lsem], pid, rid, sum(1 << e for e in engs))
+        count[lsem] = len(engs)
+        clock[(lsem, len(engs))] = dict(known["g"])
+        note(lsem, (lsem, len(engs)), [R(src)], [])
+
+    for t in range(STEPS):
+        for buf, sem in (("zl", "za"), ("yl", "ya")):
+            hist[buf + str(t)] = [("remote", (sem + str(t), NENG), 0, 256, True, 1)]
+            count[sem + str(t)] = NENG
+
+    V, S, TE = g.vector, g.scalar, g.tensor
+
+    def tt(out, a, b, op):
+        emit("v", lambda: V.tensor_tensor(ap(out), ap(a), ap(b), op), [a, b], [out])
+
+    def ts(out, a, s1, op0, s2=None, op1=None):
+        rs = [a] + [s for s in (s1, s2) if not isinstance(s, (int, float)) and s is not None]
+        c1 = s1 if isinstance(s1, (int, float)) else ap(s1)
+        if op1 is None:
+            emit("v", lambda: V.tensor_scalar(ap(out), ap(a), c1, None, op0), rs, [out])
+        else:
+            c2 = s2 if isinstance(s2, (int, float)) else ap(s2)
+            emit("v", lambda: V.tensor_scalar(ap(out), ap(a), c1, c2, op0, op1), rs, [out])
+
+    def cp(out, a):
+        emit("v", lambda: V.tensor_copy(ap(out), ap(a)), [a], [out])
+
+    def fill(out, c):
+        emit("v", lambda: V.memset(ap(out), c), [], [out])
+
+    def scan(out, d0, d1):
+        emit("v", lambda: V.tensor_tensor_scan(ap(out), ap(d0), ap(d1), 0.0, A.mult, A.max), [d0, d1], [out])
+
+    def act(out, a, f, bias=0.0, scale=1.0):
+        emit("s", lambda: S.activation(ap(out), ap(a), f, bias=bias, scale=scale), [a], [out])
+
+    def mm(out, lhsT, rhs, start=True, stop=True):
+        emit("t", lambda: TE.matmul(ap(out), ap(lhsT), ap(rhs), start, stop), [lhsT, rhs], [out])
+
+    def aff(out, a, pat, op, fl, base, cm):
+        emit("g", lambda: g.affine_select(ap(out), ap(a), pat, op, fl, base, cm), [a], [out])
+
+    def iota(out, pat, base, cm):
+        emit("g", lambda: g.iota(ap(out), pat, base, cm, allow_small_or_imprecise_dtypes=True), [], [out])
+
+    dma("y", T.sp[:], T.spot[:], [], [R("sp")])
+    dma("y", T.KI[:], T.kids[:], [], [R("KI")])
+    dma("s", T.wt[:], T.wts[:], [], [R("wt")])
+    dma("s", T.x0[:], T.cand[:], [], [R("x0")])
+    dma("s", T.XT[:, 0:M], T.nodes[:], [], [R("XT", 0, M)])
+    dma("y", T.BK[:], T.book[:], [], [R("BK")])
+
+    fill(R("ONE"), 1.0)
+    fill(R("ZER"), 0.0)
+    aff(R("IDb"), R("ONE", 0, 128), [[-1, 128]], A.is_equal, 0.0, 0, 1)
+    aff(R("G8t"), R("ONE", 0, 8), [[-16, 8]], A.is_ge, 0.0, 0, 1)
+    aff(R("G8"), R("G8t"), [[16, 8]], A.is_ge, 0.0, 15, -1)
+    fill(R("W1"), 0.0)
+    fill(R("W2"), 0.0)
+    fill(R("XT", M, 4096), 0.0)
+    ts(R("NIDb"), R("IDb"), -1.0, A.mult)
+    for m in range(16):
+        cp(R("REP", m, 2048, 16), R("IDb"))
+    cp(R("G8f"), R("G8"))
+    cp(R("lvu"), R("sp"))
+    cp(R("lv0"), R("sp"))
+    for j, w in ((0, "W1"), (1, "W2")):
+        ts(R("GW", 8 * j, 8 * j + 8), R("G8f"), R("wt", j, j + 1), A.mult)
+        for q in range(8):
+            ts(R(w, 16 * q, 16 * q + 129 * 15 + 1, 129), R("ONE", 0, 16), R("GW", 8 * j + q, 8 * j + q + 1), A.mult)
+    aff(R("PK8"), R("ONE", 0, 8), [[-16, 8]], A.is_equal, 0.0, 0, 1)
+    aff(R("TRI"), R("ZER"), [[1, 128]], A.is_gt, -8192.0, 0, -1)
+    iota(R("IDX"), [[1, 2304]], -1280, 0)
+    fill(R("CR"), 0.0)
+    fill(R("CR", 128, 256, 1, 2), 2048.0)
+    fill(R("CR", 256, 384, 1, 2), 1.0)
+    fill(R("CR", 256, 384, 1, 1), -2048.0)
+    iota(R("CR", 128, 256, 1, 1), [[0, 8], [-4096, 16]], 65536, 0)
+    iota(R("II"), [[1, 256]], M - 4095, 0)
+    iota(R("trash"), [[16, 16]], W, 1)
+
+    def more_constants():
+        cp(R("IDf"), R("IDb"))
+        ts(R("NIDf"), R("IDb"), -1.0, A.mult)
+        ts(R("N20"), R("IDb"), -float(2 ** 20), A.mult)
+        ts(R("N22"), R("IDb"), -float(2 ** 22), A.mult)
+        ts(R("I4K"), R("IDb"), 4096.0, A.mult)
+        for z, c in ((0, 4096.0), (8, 65536.0), (16, 4096.0)):
+            ts(R("GS", z, z + 8), R("G8"), c, A.mult)
+        ts(R("GO"), R("G8"), -float(2 ** 19), A.mult)
+        tt(R("pms", 0, 64), R("IDb", 0, 64), R("IDb", 64, 128), A.add)
+        tt(R("pms", 64, 96), R("pms", 0, 32), R("pms", 32, 64), A.add)
+        tt(R("pm", 0, 16), R("pms", 64, 80), R("pms", 80, 96), A.add)
+        for n in (16, 32, 64, 128):
+            cp(R("pm", n, 2 * n), R("pm", 0, n))
+        ts(R("npm"), R("pm"), -1.0, A.mult, 1.0, A.add)
+
+    def even_more():
+        ts(R("pmn"), R("pm"), BIG + 1.0, A.mult, -BIG, A.add)
+        ts(R("pm256"), R("pm"), 256.0, A.mult)
+        fill(R("rmf"), 1.0)
+        fill(R("rmb"), 1.0)
+        ts(R("rmf", 0, 128, 16), R("ONE", 0, 8), 0.0, A.mult)
+        ts(R("rmb", 0, 128, 16), R("ONE", 0, 8), 0.0, A.mult)
+        tt(R("CA0"), R("pm"), R("II"), A.mult)
+        ts(R("CA0"), R("CA0"), 4095.0, A.add)
+        cp(R("ET", 0, M), R("KI"))
+        fill(R("ET", M, W), 4095.0)
+
+    def hash_ops(u, n, ui, p, out):
+        cp(R(ui, 0, 2 * n), u)
+        ts(R(ui, 0, 2 * n), R(ui, 0, 2 * n), 4095, A.bitwise_and)
+        tt(R(p, 0, n), R(ui, 0, n), R(ui, n, 2 * n), A.mult)
+        ts(R(p, 0, n), R(p, 0, n), 5, A.arith_shift_right)
+        tt(R(p, 0, n), R(p, 0, n), R(ui, n, 2 * n), A.add)
+        ts(R(p, 0, n), R(p, 0, n), 4095, A.bitwise_and)
+        cp(out, R(p, 0, n))
+
+    for t in range(STEPS):
+        x, xn = ("x0", "x1") if t % 2 == 0 else ("x1", "x0")
+        lv, lvn = ("lv0", "lv1") if t % 2 == 0 else ("lv1", "lv0")
+        CA, CAn = ("CA0", "CA1") if t % 2 == 0 else ("CA1", "CA0")
+        st = str(t)
+        last = t == STEPS - 1
+        tab = ("KI", M) if t == 0 else ("ET", M + 256 * (t - 1))
+
+        def G1(c):
+            act(R("XG", 1024 * c, 1024 * c + 1024), P("ind", R("XT"), R("CL", 64 * c, 64 * c + 64)), F.Copy)
+
+        def sub(c):
+            for b in range(2):
+                j = 2 * c + b
+                h = j // 4
+                mm(R("dp%d" % b), R("NIDb"), R("XG", 512 * j, 512 * j + 512), True, False)
+                mm(R("dp%d" % b), R("xT", 128 * h, 128 * h + 128), R("REP", 512 * (j % 4), 512 * (j % 4) + 512), False, True)
+
+        def AS(c):
+            for b in range(2):
+                o = 1024 * c + 512 * b
+                act(R("DD", o, o + 512), R("dp%d" % b), F.Abs)
+                act(R("SG", o, o + 512), R("dp%d" % b), F.Sign, 0.5)
+
+        def hashes(c):
+            for u, w in ((0, "W1"), (64, "W2")):
+                for k in range(16):
+                    mm(R("up", u, u + 64), R(w, 128 * k, 128 * k + 128), R("DD", 1024 * c + k, 1024 * c + 1024, 16), k == 0, k == 15)
+
+        def vhash(c):
+            hash_ops(R("up", 0, 128), 64, "hu", "hp", R("HL", 64 * c, 64 * c + 64))
+
+        def G2(c):
+            o = 1024 * c
+            tt(R("CMP", o, o + 1024), P("ind", R("BK"), R("HL", 64 * c, 64 * c + 64)), R("DD", o, o + 1024), A.is_ge)
+
+        def over(h):
+            for k in range(16):
+                mm(R("ov", 128 * h + k, 128 * h + 128, 16), R("SG", 2048 * h + k, 2048 * h + 2048, 16), R("GO"))
+            ts(R("tA", 128 * h, 128 * h + 128), R("ov", 128 * h, 128 * h + 128), 11.5 * 2 ** 20 - BIG, A.add, 4095.0, A.max)
+
+        def scount(h):
+            for k in range(16):
+                mm(R("BH%d" % h, k, 384, 16), R("CMP", 2048 * h + k, 2048 * h + 2048, 16), R("GS"), False, k == 15)
+
+        def bh_open(h):
+            b = "BH%d" % h
+            hs = (128 * h, 128 * h + 128)
+            mm(R(b), R("ONE", 0, 128), R("CR"), True, False)
+            mm(R(b, 0, 128), R("Ff", *hs), R("NIDf"), False, False)
+            mm(R(b, 0, 128), R("em", *hs), R("N20"), False, False)
+            mm(R(b, 128, 256), R("Cm", *hs), R("IDb"), False, False)
+            mm(R(b, 128, 256), R("em", *hs), R("N22"), False, False)
+            mm(R(b, 256, 384), R("Cm", *hs), R("IDb"), False, False)
+            mm(R(b, 384, 512), R("Rm", *hs), R("IDf"), False, False)
+
+        def same(q):
+            b = "m%d" % (q % 2)
+            pk = R("PICK", 128 * q, 128 * q + 128)
+            mm(R(b, 0, 128), R("IDb"), R("TRI"), True, False)
+            mm(R(b, 0, 128), pk, R("vA", 0, 128), False, True)
+            mm(R(b, 128, 256), pk, R("vA", 128, 256))
+            mm(R(b, 256, 384), R("IDb"), R("TRI"), True, False)
+            mm(R(b, 256, 384), pk, R("vA", 128, 256), False, True)
+            o = 384 * q
+            ts(R("MQ", o, o + 256), R(b, 0, 256), R("vcol", q, q + 1), A.is_equal)
+            ts(R("MQ", o + 256, o + 384), R(b, 256, 384), R("vcol", 8 + q, 9 + q), A.is_equal)
+
+        def decide(h):
+            b = "BH%d" % h
+            lo, hi = 128 * h, 128 * h + 128
+
+            def r(n, step=1):
+                return R(n, lo, hi, step)
+            tt(r("cap"), R(b, 0, 128), r("tA"), A.is_gt)
+            ts(r("nc"), r("cap"), -1.0, A.mult, 1.0, A.add)
+            tt(r("key"), r("nc"), R(b, 128, 256), A.mult)
+            tt(r("wm"), r("pmn"), r("key"), A.is_gt)
+            scan(r("w1s"), R("rmb"), r("wm"))
+            scan(r("wb", -1), R("rmb"), r("w1s", -1))
+
+        def decide2(h):
+            b = "BH%d" % h
+            lo, hi = 128 * h, 128 * h + 128
+
+            def r(n, step=1):
+                return R(n, lo, hi, step)
+            tt(r("r2"), r("nc"), R(b, 384, 512), A.mult)
+            tt(r("NE"), r("cap"), R(b, 256, 384), A.mult)
+            scan(r("n1"), R("rmf"), r("NE"))
+            scan(r("n2", -1), R("rmf"), r("n1", -1))
+            ts(r("Si"), r("n2"), 2.0 ** -12, A.mult, 0.5 - 2.0 ** -13, A.add)
+            tt(r("pS"), r("Si"), r("pm"), A.mult)
+            scan(r("k1"), R("rmf"), r("key"))
+            scan(r("k2", -1), R("rmf"), r("k1", -1))
+            tt(r("dpm"), r("k2"), r("pm"), A.mult)
+
+        cp(R("Ei"), P("ind", R(tab[0], 0, tab[1]), R("lvu")))
+        ts(R("Ci"), R("Ei"), 4095, A.bitwise_and)
+        cp(R("CL"), R("Ci"))
+        tt(R("d0"), P("ind", R("XT"), R("lvu")), R(x), A.subtract)
+        for h in range(2):
+            mm(R("m0", 128 * h, 128 * h + 128), R(x, 128 * h, 128 * h + 128), R("IDb"))
+        cp(R("xT"), R("m0", 0, 256))
+        G1(0)
+        act(R("z" + st), R("d0"), F.Abs)
+        send("z" + st, "zl" + st, (rank + 1 + t) % 4, "zs" + st, "za" + st)
+        sub(0)
+        G1(1)
+        AS(0)
+        if t == 0:
+            aff(R("PICK"), R("ONE"), [[-16, 8], [0, 128]], A.is_equal, 0.0, 0, 1)
+            more_constants()
+        ts(R("Ff"), R("Ei"), -4095.0, A.add)
+        ts(R("em"), R("Ci"), 4095.0, A.is_equal)
+        ts(R("Cm"), R("Ci"), -2048.0, A.add)
+        tt(R("Rm"), R("Ff"), R("npm"), A.mult)
+        cp(R("vA"), P("ind", R("IDX"), R("lvu")))
+        hashes(0)
+        bh_open(0)
+        for h in range(2):
+            mm(R("m1", 8 * h, 8 * h + 8), R("vA", 128 * h, 128 * h + 128), R("PK8"))
+        cp(R("vcol"), R("m1", 0, 16))
+        vhash(0)
+        G2(0)
+        same(0)
+        same(1)
+        G1(2)
+        sub(1)
+        AS(1)
+        bh_open(1)
+        hashes(1)
+        if t == 0:
+            even_more()
+        vhash(1)
+        G2(1)
+        over(0)
+        scount(0)
+        same(2)
+        same(3)
+        G1(3)
+        sub(2)
+        AS(2)
+        hashes(2)
+        for u, w in ((256, "W1"), (272, "W2")):
+            for m in range(16):
+                mm(R("up", u, u + 16), R(w, 128 * m, 128 * m + 128), R("zl" + st, m, 256, 16), m == 0, m == 15)
+        vhash(2)
+        hash_ops(R("up", 256, 288), 16, "ru", "rp", R("rl"))
+        G2(2)
+        same(4)
+        same(5)
+        decide(0)
+        sub(3)
+        AS(3)
+        act(R("yr" + st), P("ind", R("BK"), R("rl")), F.Copy)
+        send("yr" + st, "yl" + st, (rank - 1 - t) % 4, "ys" + st, "ya" + st)
+        hashes(3)
+        vhash(3)
+        G2(3)
+        over(1)
+        scount(1)
+        same(6)
+        same(7)
+        decide2(0)
+        mm(R("dp0", 0, 256), R("IDb"), R("yl" + st), True, False)
+        mm(R("dp0", 0, 256), R("NIDb"), R(x), False, True)
+        act(R("rr"), R("dp0", 0, 256), F.Abs)
+        mm(R("dp0", 256, 512), R("IDb"), R("rr"), True, False)
+        mm(R("dp0", 256, 512), R("NIDb"), R(x), False, True)
+        act(R("rx"), R("dp0", 256, 512), F.Copy)
+        decide(1)
+        for hi in range(2):
+            for q in range(8):
+                o = 256 + 128 * hi + 16 * q
+                mm(R("ov", o, o + 16), R("MQ", 384 * q + 128 * hi, 384 * q + 128 * hi + 128), R("wb", 16 * q, 16 * q + 16), True, hi == 0)
+                if hi == 1:
+                    mm(R("ov", o, o + 16), R("MQ", 384 * q + 256, 384 * q + 384), R("wb", 128 + 16 * q, 144 + 16 * q), False, True)
+        decide2(1)
+        tt(R("winb"), R("ov", 256, 512), R("wb"), A.is_lt)
+        tt(R("winm"), R("ov", 256, 512), R("wm"), A.is_lt)
+        for h in range(2):
+            hs = (128 * h, 128 * h + 128)
+            mm(R("dp1", *hs), R("winb", *hs), R("IDb"))
+        for h in range(2):
+            hs = (128 * h, 128 * h + 128)
+            mm(R("up", 128 + 8 * h, 136 + 8 * h), R("wm", *hs), R("G8"))
+            mm(R("up", 144 + 8 * h, 152 + 8 * h), R("winm", *hs), R("G8"))
+            mm(R("up", 160 + 8 * h, 168 + 8 * h), R("dpm", *hs), R("G8f"))
+        for h in range(2):
+            hs = (128 * h, 128 * h + 128)
+            mm(R("m0", *hs), R("r2", *hs), R("IDf"), True, False)
+            mm(R("m0", *hs), R("pS", *hs), R("I4K"), False, True)
+        for h in range(2):
+            hs = (128 * h, 128 * h + 128)
+            mm(R("m1", *hs), R("NE", *hs), R("IDf"))
+        act(R("NEs"), R("m1", 0, 256), F.Copy)
+        tt(R("dp0", 0, 256), R("rx"), R("dp1", 0, 256), A.mult)
+        tt(R(xn), R("dp0", 0, 256), R(x), A.add)
+        for m in range(16):
+            mm(R("m1", 256, 272), R("W1", 128 * m, 128 * m + 128), R(xn, m, 256, 16), m == 0, m == 15)
+        tt(R("newc"), R("m0", 0, 256), R(CA), A.add)
+        cp(R("ws"), R("up", 128, 160))
+        tt(R("vt"), R(lv), R("trash"), A.subtract)
+        tt(R("of"), R("ws", 16, 32), R("vt"), A.mult)
+        tt(R("of"), R("of"), R("trash"), A.add)
+        cp(R("ofu"), R("of"))
+        cp(P("ind", R("ET", 0, 2944), R("ofu")), R("newc"))
+        n0 = M + 256 * t
+        tt(R("XT", n0, n0 + 256), R(x), R("dp1", 0, 256), A.mult)
+        tt(R("NEw"), R("NEs"), R("dp1", 0, 256), A.mult)
+        act(R("ET", n0, n0 + 256), R("NEw"), F.Identity, 4095.0)
+        cp(R("dn"), R("up", 160, 176))
+        ts(R("dn"), R("dn"), 4095, A.bitwise_and)
+        tt(R("b1"), R(lv), R("dn"), A.subtract)
+        tt(R("b1"), R("b1"), R("ws", 0, 16), A.mult)
+        tt(R("b1"), R("b1"), R("dn"), A.add)
+        cp(R("bi"), R("m1", 256, 272))
+        ts(R("bk"), R("bi"), 1023, A.bitwise_and)
+        tt(R("b2"), R("bk"), R(lv), A.subtract)
+        tt(R("b2"), R("b2"), R("ws", 16, 32), A.mult)
+        tt(R(lvn), R("b1"), R("b2"), A.add)
+        if not last:
+            cp(R("lvu"), R(lvn))
+            tt(R(CAn), R(CA), R("pm256"), A.add)
+        else:
+            dma("y", T.ykids[:], T.ET[:, 0:W], [R("ET", 0, W)], [])
+            dma("s", T.ycand[:], T[xn][:], [R(xn)], [])
+            dma("s", T.ynodes[:], T.XT[:, M:W], [R("XT", M, W)], [])
+            dma("s", T.yspot[:], T[lvn][:], [R(lvn)], [])
+
+    for sem in sorted(count):
+        need("g", (sem, count[sem]))

@@ -35,6 +35,85 @@ NDMA = 10
 SEMAPHORES = ["qv", "qs", "qt", "qg"] + ["D%d" % i for i in range(NDMA)] + [n + str(t) for t in range(STEPS) for n in ("zs", "za", "ys", "ya")]
 
 
+ORDER = {}
+CYC = 0.83e-3
+PECYC = 0.55e-3
+
+
+def overlap(a, b):
+    return a[1] < b[2] and b[1] < a[2] and not (a[3] == b[3] and a[3] > 1 and (a[1] - b[1]) % a[3])
+
+
+def schedule(nodes, psum):
+    wake = 0.1
+    n = len(nodes)
+    preds = [[] for _ in range(n)]
+    hist = {}
+    for i in range(n):
+        kind, q, fn, reads, writes, cost, sem = nodes[i]
+        seen = {}
+        for rs, w in ((reads, False), (writes, True)):
+            for r in rs:
+                bank = r[0] in psum
+                for (j, rj, wj) in hist.get(r[0], ()):
+                    ov = overlap(r, rj)
+                    same = nodes[j][1] == q and kind == "c" and nodes[j][0] == "c"
+                    if bank and (q == "t" or not same):
+                        full = not same or (ov and wj and q != "t")
+                    elif ov and (w or wj):
+                        full = not same or wj
+                    else:
+                        continue
+                    seen[j] = seen.get(j, False) or full
+        preds[i] = list(seen.items())
+        for rs, w in ((reads, False), (writes, True)):
+            for r in rs:
+                h = hist.get(r[0], [])
+                if w and abs(r[3]) == 1 and r[4] == 128 and r[0] not in psum:
+                    h = [e for e in h if not (r[1] <= e[1][1] and e[1][2] <= r[2])]
+                if r[0] in psum and len(h) > 40:
+                    h = h[-40:]
+                hist[r[0]] = h + [(i, r, w)]
+    succ = [[] for _ in range(n)]
+    for i in range(n):
+        for j, full in preds[i]:
+            succ[j].append((i, full))
+    prio = [0.0] * n
+    for i in range(n - 1, -1, -1):
+        c = nodes[i][5]
+        prio[i] = max([c] + [prio[k] + (c + wake if full else 0.0) for k, full in succ[i]])
+        if nodes[i][0] == "d":
+            prio[i] += 1e7 - 1e3 * i
+    left = [len(p) for p in preds]
+    ready = {}
+    free = {}
+    est = [0.0] * n
+    for i in range(n):
+        if not left[i]:
+            ready.setdefault(nodes[i][1], []).append(i)
+    order = []
+    while len(order) < n:
+        best = None
+        for q, r in ready.items():
+            if r:
+                t = min(max(est[i], free.get(q, 0.0)) for i in r)
+                if best is None or t < best[0]:
+                    best = (t, q)
+        t, q = best
+        i = max((k for k in ready[q] if max(est[k], free.get(q, 0.0)) <= t + 0.02), key=lambda k: (prio[k], -k))
+        ready[q].remove(i)
+        st = max(est[i], free.get(q, 0.0))
+        end = st + nodes[i][5]
+        free[q] = end if nodes[i][0] == "c" else st + (0.1 if nodes[i][0] == "d" else 1.0)
+        order.append(i)
+        for k, full in succ[i]:
+            est[k] = max(est[k], end + wake if full else st)
+            left[k] -= 1
+            if not left[k]:
+                ready.setdefault(nodes[k][1], []).append(k)
+    return order
+
+
 def rank_program(g, core, T, topo):
     rank = T.rank_of(core)
     if rank is None:
@@ -105,77 +184,116 @@ def rank_program(g, core, T, topo):
                     old = [e for e in old if not (e[0] == me and e[2:] == (r[1], r[2], w, abs(r[3])))]
                 hist[r[0]] = old + [(me, ev, r[1], r[2], w, abs(r[3]))]
 
-    def emit(q, fn, reads, writes):
-        reads, writes = flat(reads), flat(writes)
-        deps(q, q, reads, writes)
-        ins = fn()
-        sem = "q" + q
-        count[sem] = count.get(sem, 0) + 1
-        ins.then_inc(T.sem[sem], 1)
-        ev = (sem, count[sem])
-        clock[ev] = dict(known[q])
-        note(q, ev, reads, writes)
+    nodes = []
+
+    def emit(q, fn, reads, writes, cost):
+        nodes.append(("c", q, fn, flat(reads), flat(writes), cost, None))
 
     nd = [0]
 
     def dma(q, out, in_, reads, writes):
         sem = "D%d" % nd[0]
         nd[0] += 1
-        deps(q, sem, reads, writes)
-        queues[q].dma_start(out, in_).then_inc(T.sem[sem], 16)
-        count[sem] = 16
-        clock[(sem, 16)] = dict(known[q])
-        note(sem, (sem, 16), reads, writes)
+        size = 128 * (writes or reads)[0][2] * 4
+        nodes.append(("d", q, lambda: queues[q].dma_start(out, in_), reads, writes, 2.0 + size / 2.0e5, sem))
 
     def send(src, dst, peer, lsem, rsem):
         to = T.cores[peer]
         rid, pid = topo.addr(to)[:2]
         engs = topo.engines(core, to)[:NENG]
-        deps("g", lsem, [R(src)], [])
-        g.remote_dma(T[dst][:], T[src][:], T.sem[rsem], T.sem[lsem], pid, rid, sum(1 << e for e in engs))
-        count[lsem] = len(engs)
-        clock[(lsem, len(engs))] = dict(known["g"])
-        note(lsem, (lsem, len(engs)), [R(src)], [])
+
+        def fn():
+            g.remote_dma(T[dst][:], T[src][:], T.sem[rsem], T.sem[lsem], pid, rid, sum(1 << e for e in engs))
+        nodes.append(("r", "g", fn, [R(src)], [R(dst)], 5.0, (lsem, len(engs))))
+
+    def finish():
+        order = ORDER.get("order")
+        if order is None or len(order) != len(nodes):
+            order = schedule(nodes, PS)
+            ORDER["order"] = order
+        for i in order:
+            kind, q, fn, reads, writes, cost, sem = nodes[i]
+            if kind == "c":
+                deps(q, q, reads, writes)
+                name = "q" + q
+                count[name] = count.get(name, 0) + 1
+                fn().then_inc(T.sem[name], 1)
+                ev, me = (name, count[name]), q
+            elif kind == "d":
+                deps(q, sem, reads, writes)
+                fn().then_inc(T.sem[sem], 16)
+                count[sem] = 16
+                ev, me = (sem, 16), sem
+            else:
+                deps("g", sem[0], reads, [])
+                fn()
+                count[sem[0]] = sem[1]
+                ev, me, writes = sem, sem[0], []
+            clock[ev] = dict(known[q])
+            note(me, ev, reads, writes)
+        for sem in sorted(count):
+            need("g", (sem, count[sem]))
 
     for t in range(STEPS):
         for buf, sem in (("zl", "za"), ("yl", "ya")):
             hist[buf + str(t)] = [("remote", (sem + str(t), NENG), 0, 256, True, 1)]
             count[sem + str(t)] = NENG
 
+    def width(r):
+        return 16 * width(r[2]) if r[0] == "ind" else -((r[1] - r[2]) // abs(r[3]))
+
+    def dtype_of(r):
+        return "float32" if r[0] in PS else SB[r[0]][1]
+
+    def vcost(out, ins, kind):
+        if out[0] == "ind":
+            return 0.05 + 4.0 * width(out[2]) * 16 * CYC
+        n = width(out)
+        if any(r[0] == "ind" for r in ins):
+            return 0.05 + 1.56 * n * CYC
+        if kind == 2:
+            c = n if any(r[0] in PS for r in ins) else 2 * n
+        else:
+            c = n
+            if kind == 1 and all(dtype_of(r) not in ("float32", "int32") for r in [out] + ins if width(r) > 1):
+                c = n / 2
+        return max(64, c) * CYC
+
     V, S, TE = g.vector, g.scalar, g.tensor
 
     def tt(out, a, b, op):
-        emit("v", lambda: V.tensor_tensor(ap(out), ap(a), ap(b), op), [a, b], [out])
+        emit("v", lambda: V.tensor_tensor(ap(out), ap(a), ap(b), op), [a, b], [out], vcost(out, [a, b], 2))
 
     def ts(out, a, s1, op0, s2=None, op1=None):
         rs = [a] + [s for s in (s1, s2) if not isinstance(s, (int, float)) and s is not None]
         c1 = s1 if isinstance(s1, (int, float)) else ap(s1)
         if op1 is None:
-            emit("v", lambda: V.tensor_scalar(ap(out), ap(a), c1, None, op0), rs, [out])
+            emit("v", lambda: V.tensor_scalar(ap(out), ap(a), c1, None, op0), rs, [out], vcost(out, [a], 1))
         else:
             c2 = s2 if isinstance(s2, (int, float)) else ap(s2)
-            emit("v", lambda: V.tensor_scalar(ap(out), ap(a), c1, c2, op0, op1), rs, [out])
+            emit("v", lambda: V.tensor_scalar(ap(out), ap(a), c1, c2, op0, op1), rs, [out], vcost(out, [a], 1))
 
     def cp(out, a):
-        emit("v", lambda: V.tensor_copy(ap(out), ap(a)), [a], [out])
+        emit("v", lambda: V.tensor_copy(ap(out), ap(a)), [a], [out], vcost(out, [a], 1))
 
     def fill(out, c):
-        emit("v", lambda: V.memset(ap(out), c), [], [out])
+        emit("v", lambda: V.memset(ap(out), c), [], [out], vcost(out, [], 1))
 
     def scan(out, d0, d1):
-        emit("v", lambda: V.tensor_tensor_scan(ap(out), ap(d0), ap(d1), 0.0, A.mult, A.max), [d0, d1], [out])
+        emit("v", lambda: V.tensor_tensor_scan(ap(out), ap(d0), ap(d1), 0.0, A.mult, A.max), [d0, d1], [out], vcost(out, [d0, d1], 1))
 
     def act(out, a, f, bias=0.0, scale=1.0):
-        emit("s", lambda: S.activation(ap(out), ap(a), f, bias=bias, scale=scale), [a], [out])
+        emit("s", lambda: S.activation(ap(out), ap(a), f, bias=bias, scale=scale), [a], [out], vcost(out, [a], 0))
 
     def mm(out, lhsT, rhs, start=True, stop=True):
-        emit("t", lambda: TE.matmul(ap(out), ap(lhsT), ap(rhs), start, stop), [lhsT, rhs], [out])
+        cost = max(64, width(rhs)) * (4 if dtype_of(lhsT) == "float32" else 1) * PECYC
+        emit("t", lambda: TE.matmul(ap(out), ap(lhsT), ap(rhs), start, stop), [lhsT, rhs], [out], cost)
 
     def aff(out, a, pat, op, fl, base, cm):
-        emit("g", lambda: g.affine_select(ap(out), ap(a), pat, op, fl, base, cm), [a], [out])
+        emit("g", lambda: g.affine_select(ap(out), ap(a), pat, op, fl, base, cm), [a], [out], 0.17 + 2 * width(out) * CYC)
 
     def iota(out, pat, base, cm):
-        emit("g", lambda: g.iota(ap(out), pat, base, cm, allow_small_or_imprecise_dtypes=True), [], [out])
+        emit("g", lambda: g.iota(ap(out), pat, base, cm, allow_small_or_imprecise_dtypes=True), [], [out], 0.13 + 2 * width(out) * CYC)
 
     dma("y", T.sp[:], T.spot[:], [], [R("sp")])
     dma("y", T.KI[:], T.kids[:], [], [R("KI")])
@@ -481,5 +599,4 @@ def rank_program(g, core, T, topo):
             dma("s", T.ynodes[:], T.XT[:, M:W], [R("XT", M, W)], [])
             dma("s", T.yspot[:], T[lvn][:], [R(lvn)], [])
 
-    for sem in sorted(count):
-        need("g", (sem, count[sem]))
+    finish()

@@ -9,20 +9,20 @@ SB = {
     "XT": (4096, "bfloat16"), "BK": (4096, "bfloat16"), "ET": (2944, "float32"), "KI": (M, "int32"), "IDX": (2304, "float32"),
     "ONE": (1024, "bfloat16"), "ZER": (128, "bfloat16"), "IDb": (128, "bfloat16"), "NIDb": (128, "bfloat16"), "IDf": (128, "float32"), "NIDf": (128, "float32"),
     "N20": (128, "bfloat16"), "N22": (128, "bfloat16"), "I4K": (128, "bfloat16"), "G8t": (8, "bfloat16"), "G8": (8, "bfloat16"), "G8f": (8, "float32"),
-    "GW": (16, "float32"), "W1": (2048, "bfloat16"), "W2": (2048, "bfloat16"), "GS": (24, "bfloat16"), "GO": (8, "bfloat16"),
+    "GW": (16, "float32"), "W1": (2048, "bfloat16"), "W2": (2048, "bfloat16"), "GS": (24, "bfloat16"), "GO": (8, "bfloat16"), "GO2": (8, "bfloat16"),
     "PICK": (1024, "bfloat16"), "PK8": (8, "bfloat16"), "TRI": (128, "bfloat16"), "pms": (128, "bfloat16"), "pm": (256, "bfloat16"), "npm": (256, "bfloat16"),
     "pmn": (256, "float32"), "rmf": (128, "float32"), "rmb": (128, "bfloat16"), "CR": (512, "bfloat16"), "REP": (2048, "bfloat16"), "trash": (16, "float32"),
-    "II": (256, "float32"), "CA0": (256, "float32"), "CA1": (256, "float32"), "pm256": (256, "float32"),
+    "II": (256, "bfloat16"), "pmI": (256, "bfloat16"), "cI0": (128, "bfloat16"), "cI1": (128, "bfloat16"), "cI2": (128, "bfloat16"),
     "wt": (2, "bfloat16"), "sp": (16, "int32"), "x0": (256, "bfloat16"), "x1": (256, "bfloat16"), "lv0": (16, "float32"), "lv1": (16, "float32"), "lvu": (16, "uint16"),
     "Ei": (256, "int32"), "Ci": (256, "int32"), "CL": (256, "uint16"), "Ff": (256, "float32"), "em": (256, "bfloat16"), "Cm": (256, "float16"), "Rm": (256, "float32"),
     "vA": (256, "float16"), "vcol": (16, "float32"), "xT": (256, "bfloat16"), "d0": (256, "bfloat16"),
     "XG": (4096, "bfloat16"), "DD": (4096, "bfloat16"), "SG": (4096, "bfloat16"), "CMP": (4096, "bfloat16"), "HL": (256, "uint16"),
-    "hu": (128, "int32"), "hp": (64, "int32"), "ru": (32, "int32"), "rp": (16, "int32"), "rl": (16, "uint16"), "MQ": (3072, "bfloat16"),
+    "hu0": (256, "int32"), "hp0": (128, "int32"), "hu1": (256, "int32"), "hp1": (128, "int32"), "ru": (32, "int32"), "rp": (16, "int32"), "rl": (16, "uint16"), "MQ": (3072, "bfloat16"), "MD": (3072, "bfloat16"),
     "tA": (256, "float32"), "cap": (256, "bfloat16"), "nc": (256, "bfloat16"), "key": (256, "float32"), "wm": (256, "bfloat16"), "w1s": (256, "bfloat16"), "wb": (256, "bfloat16"),
     "k1": (256, "float32"), "k2": (256, "float32"), "dpm": (256, "float32"), "NE": (256, "float32"), "n1": (256, "float32"), "n2": (256, "float32"), "Si": (256, "int32"), "pS": (256, "bfloat16"),
     "r2": (256, "float32"), "winb": (256, "bfloat16"), "winm": (256, "bfloat16"), "newc": (256, "float32"), "NEs": (256, "float32"), "NEw": (256, "float32"),
     "rr": (256, "bfloat16"), "rx": (256, "bfloat16"), "ws": (32, "float32"), "of": (16, "float32"), "ofu": (16, "uint16"), "vt": (16, "float32"),
-    "dn": (16, "int32"), "b1": (16, "float32"), "b2": (16, "float32"), "bi": (16, "int32"), "bk": (16, "int32"),
+    "dn": (16, "int32"), "bk2": (16, "float32"), "b1": (16, "float32"), "b2": (16, "float32"), "bi": (16, "int32"), "bk": (16, "int32"),
 }
 for _t in range(STEPS):
     for _n in ("z", "zl", "yr", "yl"):
@@ -37,7 +37,12 @@ SEMAPHORES = ["qv", "qs", "qt", "qg"] + ["D%d" % i for i in range(NDMA)] + [n + 
 
 ORDER = {}
 CYC = 0.83e-3
-PECYC = 0.55e-3
+PECYC = 0.45e-3
+WAKE = 0.18
+CHUNKS = ((0, 2), (2, 4), (4, 6), (6, 8))
+G1V = ()
+SGV = (0,)
+MQV = tuple(range(8))
 
 
 def overlap(a, b):
@@ -45,7 +50,7 @@ def overlap(a, b):
 
 
 def schedule(nodes, psum):
-    wake = 0.1
+    wake = WAKE
     n = len(nodes)
     preds = [[] for _ in range(n)]
     hist = {}
@@ -283,7 +288,8 @@ def rank_program(g, core, T, topo):
         emit("v", lambda: V.tensor_tensor_scan(ap(out), ap(d0), ap(d1), 0.0, A.mult, A.max), [d0, d1], [out], vcost(out, [d0, d1], 1))
 
     def act(out, a, f, bias=0.0, scale=1.0):
-        emit("s", lambda: S.activation(ap(out), ap(a), f, bias=bias, scale=scale), [a], [out], vcost(out, [a], 0))
+        col = not isinstance(bias, (int, float))
+        emit("s", lambda: S.activation(ap(out), ap(a), f, bias=ap(bias) if col else bias, scale=scale), [a] + ([bias] if col else []), [out], vcost(out, [a], 0))
 
     def mm(out, lhsT, rhs, start=True, stop=True):
         cost = max(64, width(rhs)) * (4 if dtype_of(lhsT) == "float32" else 1) * PECYC
@@ -328,7 +334,9 @@ def rank_program(g, core, T, topo):
     fill(R("CR", 256, 384, 1, 2), 1.0)
     fill(R("CR", 256, 384, 1, 1), -2048.0)
     iota(R("CR", 128, 256, 1, 1), [[0, 8], [-4096, 16]], 65536, 0)
-    iota(R("II"), [[1, 256]], M - 4095, 0)
+    iota(R("II"), [[1, 256]], 1, 0)
+    fill(R("CR", 0, 128, 1, 2), 1.0)
+    fill(R("CR", 0, 128, 1, 1), -4096.0)
     iota(R("trash"), [[16, 16]], W, 1)
 
     def more_constants():
@@ -340,6 +348,8 @@ def rank_program(g, core, T, topo):
         for z, c in ((0, 4096.0), (8, 65536.0), (16, 4096.0)):
             ts(R("GS", z, z + 8), R("G8"), c, A.mult)
         ts(R("GO"), R("G8"), -float(2 ** 19), A.mult)
+        if SGV:
+            ts(R("GO2"), R("G8"), -float(2 ** 20), A.mult)
         tt(R("pms", 0, 64), R("IDb", 0, 64), R("IDb", 64, 128), A.add)
         tt(R("pms", 64, 96), R("pms", 0, 32), R("pms", 32, 64), A.add)
         tt(R("pm", 0, 16), R("pms", 64, 80), R("pms", 80, 96), A.add)
@@ -349,13 +359,13 @@ def rank_program(g, core, T, topo):
 
     def even_more():
         ts(R("pmn"), R("pm"), BIG + 1.0, A.mult, -BIG, A.add)
-        ts(R("pm256"), R("pm"), 256.0, A.mult)
         fill(R("rmf"), 1.0)
         fill(R("rmb"), 1.0)
         ts(R("rmf", 0, 128, 16), R("ONE", 0, 8), 0.0, A.mult)
         ts(R("rmb", 0, 128, 16), R("ONE", 0, 8), 0.0, A.mult)
-        tt(R("CA0"), R("pm"), R("II"), A.mult)
-        ts(R("CA0"), R("CA0"), 4095.0, A.add)
+        tt(R("pmI"), R("pm"), R("II"), A.mult)
+        for u in range(STEPS):
+            ts(R("cI%d" % u), R("IDb"), -2304.0 + 256.0 * u, A.mult)
         cp(R("ET", 0, M), R("KI"))
         fill(R("ET", M, W), 4095.0)
 
@@ -371,43 +381,38 @@ def rank_program(g, core, T, topo):
     for t in range(STEPS):
         x, xn = ("x0", "x1") if t % 2 == 0 else ("x1", "x0")
         lv, lvn = ("lv0", "lv1") if t % 2 == 0 else ("lv1", "lv0")
-        CA, CAn = ("CA0", "CA1") if t % 2 == 0 else ("CA1", "CA0")
         st = str(t)
         last = t == STEPS - 1
         tab = ("KI", M) if t == 0 else ("ET", M + 256 * (t - 1))
 
-        def G1(c):
-            act(R("XG", 1024 * c, 1024 * c + 1024), P("ind", R("XT"), R("CL", 64 * c, 64 * c + 64)), F.Copy)
+        def G1(b0, b1):
+            if b0 in G1V:
+                cp(R("XG", 512 * b0, 512 * b1), P("ind", R("XT"), R("CL", 32 * b0, 32 * b1)))
+            else:
+                act(R("XG", 512 * b0, 512 * b1), P("ind", R("XT"), R("CL", 32 * b0, 32 * b1)), F.Copy)
 
-        def sub(c):
-            for b in range(2):
-                j = 2 * c + b
-                h = j // 4
-                mm(R("dp%d" % b), R("NIDb"), R("XG", 512 * j, 512 * j + 512), True, False)
-                mm(R("dp%d" % b), R("xT", 128 * h, 128 * h + 128), R("REP", 512 * (j % 4), 512 * (j % 4) + 512), False, True)
+        def sub(j):
+            h, b = j // 4, "dp%d" % (j % 2)
+            mm(R(b), R("NIDb"), R("XG", 512 * j, 512 * j + 512), True, False)
+            mm(R(b), R("xT", 128 * h, 128 * h + 128), R("REP", 512 * (j % 4), 512 * (j % 4) + 512), False, True)
+            act(R("DD", 512 * j, 512 * j + 512), R(b), F.Abs)
+            if h in SGV:
+                ts(R("SG", 512 * j, 512 * j + 512), R(b), 0.0, A.is_ge)
+            else:
+                act(R("SG", 512 * j, 512 * j + 512), R(b), F.Sign, 0.5)
 
-        def AS(c):
-            for b in range(2):
-                o = 1024 * c + 512 * b
-                act(R("DD", o, o + 512), R("dp%d" % b), F.Abs)
-                act(R("SG", o, o + 512), R("dp%d" % b), F.Sign, 0.5)
-
-        def hashes(c):
-            for u, w in ((0, "W1"), (64, "W2")):
+        def hashes(b0, b1, c):
+            n = 32 * (b1 - b0)
+            for u, w in ((0, "W1"), (n, "W2")):
                 for k in range(16):
-                    mm(R("up", u, u + 64), R(w, 128 * k, 128 * k + 128), R("DD", 1024 * c + k, 1024 * c + 1024, 16), k == 0, k == 15)
-
-        def vhash(c):
-            hash_ops(R("up", 0, 128), 64, "hu", "hp", R("HL", 64 * c, 64 * c + 64))
-
-        def G2(c):
-            o = 1024 * c
-            tt(R("CMP", o, o + 1024), P("ind", R("BK"), R("HL", 64 * c, 64 * c + 64)), R("DD", o, o + 1024), A.is_ge)
+                    mm(R("up", u, u + n), R(w, 128 * k, 128 * k + 128), R("DD", 512 * b0 + k, 512 * b1, 16), k == 0, k == 15)
+            hash_ops(R("up", 0, 2 * n), n, "hu%d" % (c % 2), "hp%d" % (c % 2), R("HL", 32 * b0, 32 * b1))
+            tt(R("CMP", 512 * b0, 512 * b1), P("ind", R("BK"), R("HL", 32 * b0, 32 * b1)), R("DD", 512 * b0, 512 * b1), A.is_ge)
 
         def over(h):
             for k in range(16):
-                mm(R("ov", 128 * h + k, 128 * h + 128, 16), R("SG", 2048 * h + k, 2048 * h + 2048, 16), R("GO"))
-            ts(R("tA", 128 * h, 128 * h + 128), R("ov", 128 * h, 128 * h + 128), 11.5 * 2 ** 20 - BIG, A.add, 4095.0, A.max)
+                mm(R("ov", 128 * h + k, 128 * h + 128, 16), R("SG", 2048 * h + k, 2048 * h + 2048, 16), R("GO2" if h in SGV else "GO"))
+            act(R("tA", 128 * h, 128 * h + 128), R("ov", 128 * h, 128 * h + 128), F.Relu, 11.5 * 2 ** 20 - (0.0 if h in SGV else BIG) - 4095.0)
 
         def scount(h):
             for k in range(16):
@@ -433,8 +438,14 @@ def rank_program(g, core, T, topo):
             mm(R(b, 256, 384), R("IDb"), R("TRI"), True, False)
             mm(R(b, 256, 384), pk, R("vA", 128, 256), False, True)
             o = 384 * q
-            ts(R("MQ", o, o + 256), R(b, 0, 256), R("vcol", q, q + 1), A.is_equal)
-            ts(R("MQ", o + 256, o + 384), R(b, 256, 384), R("vcol", 8 + q, 9 + q), A.is_equal)
+            if q in MQV:
+                ts(R("MQ", o, o + 256), R(b, 0, 256), R("vcol", q, q + 1), A.add, 0.0, A.is_equal)
+                ts(R("MQ", o + 256, o + 384), R(b, 256, 384), R("vcol", 8 + q, 9 + q), A.add, 0.0, A.is_equal)
+                return
+            act(R("MD", o, o + 256), R(b, 0, 256), F.Abs, R("vcol", q, q + 1))
+            act(R("MD", o + 256, o + 384), R(b, 256, 384), F.Abs, R("vcol", 8 + q, 9 + q))
+            if q % 2:
+                ts(R("MQ", o - 384, o + 384), R("MD", o - 384, o + 384), 0.0, A.is_equal)
 
         def decide(h):
             b = "BH%d" % h
@@ -443,9 +454,9 @@ def rank_program(g, core, T, topo):
             def r(n, step=1):
                 return R(n, lo, hi, step)
             tt(r("cap"), R(b, 0, 128), r("tA"), A.is_gt)
-            ts(r("nc"), r("cap"), -1.0, A.mult, 1.0, A.add)
-            tt(r("key"), r("nc"), R(b, 128, 256), A.mult)
-            tt(r("wm"), r("pmn"), r("key"), A.is_gt)
+            tt(r("nc"), R(b, 0, 128), r("tA"), A.is_le)
+            tt(R(b, 128, 256), r("nc"), R(b, 128, 256), A.mult)
+            tt(r("wm"), r("pmn"), R(b, 128, 256), A.is_gt)
             scan(r("w1s"), R("rmb"), r("wm"))
             scan(r("wb", -1), R("rmb"), r("w1s", -1))
 
@@ -461,23 +472,22 @@ def rank_program(g, core, T, topo):
             scan(r("n2", -1), R("rmf"), r("n1", -1))
             ts(r("Si"), r("n2"), 2.0 ** -12, A.mult, 0.5 - 2.0 ** -13, A.add)
             tt(r("pS"), r("Si"), r("pm"), A.mult)
-            scan(r("k1"), R("rmf"), r("key"))
-            scan(r("k2", -1), R("rmf"), r("k1", -1))
-            tt(r("dpm"), r("k2"), r("pm"), A.mult)
+            scan(r("k1"), R("rmf"), R(b, 128, 256))
+            scan(R(b, 128, 256, -1), R("rmf"), r("k1", -1))
+            tt(r("dpm"), r("pm"), R(b, 128, 256), A.mult)
 
-        cp(R("Ei"), P("ind", R(tab[0], 0, tab[1]), R("lvu")))
-        ts(R("Ci"), R("Ei"), 4095, A.bitwise_and)
-        cp(R("CL"), R("Ci"))
+        for a, b in ((0, 64), (64, 256)):
+            cp(R("Ei", a, b), P("ind", R(tab[0], 0, tab[1]), R("lvu", a // 16, b // 16)))
+            ts(R("Ci", a, b), R("Ei", a, b), 4095, A.bitwise_and)
+            cp(R("CL", a, b), R("Ci", a, b))
         tt(R("d0"), P("ind", R("XT"), R("lvu")), R(x), A.subtract)
         for h in range(2):
             mm(R("m0", 128 * h, 128 * h + 128), R(x, 128 * h, 128 * h + 128), R("IDb"))
-        cp(R("xT"), R("m0", 0, 256))
-        G1(0)
+        act(R("xT"), R("m0", 0, 256), F.Copy)
         act(R("z" + st), R("d0"), F.Abs)
         send("z" + st, "zl" + st, (rank + 1 + t) % 4, "zs" + st, "za" + st)
-        sub(0)
-        G1(1)
-        AS(0)
+        for b0, b1 in CHUNKS:
+            G1(b0, b1)
         if t == 0:
             aff(R("PICK"), R("ONE"), [[-16, 8], [0, 128]], A.is_equal, 0.0, 0, 1)
             more_constants()
@@ -486,56 +496,40 @@ def rank_program(g, core, T, topo):
         ts(R("Cm"), R("Ci"), -2048.0, A.add)
         tt(R("Rm"), R("Ff"), R("npm"), A.mult)
         cp(R("vA"), P("ind", R("IDX"), R("lvu")))
-        hashes(0)
-        bh_open(0)
         for h in range(2):
             mm(R("m1", 8 * h, 8 * h + 8), R("vA", 128 * h, 128 * h + 128), R("PK8"))
-        cp(R("vcol"), R("m1", 0, 16))
-        vhash(0)
-        G2(0)
-        same(0)
-        same(1)
-        G1(2)
-        sub(1)
-        AS(1)
+        ts(R("vcol"), R("m1", 0, 16), -1.0, A.mult)
+        bh_open(0)
         bh_open(1)
-        hashes(1)
         if t == 0:
             even_more()
-        vhash(1)
-        G2(1)
-        over(0)
-        scount(0)
-        same(2)
-        same(3)
-        G1(3)
-        sub(2)
-        AS(2)
-        hashes(2)
-        for u, w in ((256, "W1"), (272, "W2")):
-            for m in range(16):
-                mm(R("up", u, u + 16), R(w, 128 * m, 128 * m + 128), R("zl" + st, m, 256, 16), m == 0, m == 15)
-        vhash(2)
-        hash_ops(R("up", 256, 288), 16, "ru", "rp", R("rl"))
-        G2(2)
-        same(4)
-        same(5)
+        for c, (b0, b1) in enumerate(CHUNKS):
+            for j in range(b0, b1):
+                sub(j)
+                if j in (3, 7):
+                    over(j // 4)
+                if j == 3:
+                    for u, w in ((256, "W1"), (272, "W2")):
+                        for m in range(16):
+                            mm(R("ov", u, u + 16), R(w, 128 * m, 128 * m + 128), R("zl" + st, m, 256, 16), m == 0, m == 15)
+                    hash_ops(R("ov", 256, 288), 16, "ru", "rp", R("rl"))
+                    act(R("yr" + st), P("ind", R("BK"), R("rl")), F.Copy)
+                    send("yr" + st, "yl" + st, (rank - 1 - t) % 4, "ys" + st, "ya" + st)
+            hashes(b0, b1, c)
+            if b1 in (4, 8):
+                scount(b1 // 4 - 1)
+        for q in range(8):
+            same(q)
         decide(0)
-        sub(3)
-        AS(3)
-        act(R("yr" + st), P("ind", R("BK"), R("rl")), F.Copy)
-        send("yr" + st, "yl" + st, (rank - 1 - t) % 4, "ys" + st, "ya" + st)
-        hashes(3)
-        vhash(3)
-        G2(3)
-        over(1)
-        scount(1)
-        same(6)
-        same(7)
         decide2(0)
         mm(R("dp0", 0, 256), R("IDb"), R("yl" + st), True, False)
         mm(R("dp0", 0, 256), R("NIDb"), R(x), False, True)
         act(R("rr"), R("dp0", 0, 256), F.Abs)
+        for m in range(16):
+            mm(R("up", 384, 400), R("W1", 128 * m, 128 * m + 128), R("rr", m, 256, 16), m == 0, m == 15)
+        cp(R("bi"), R("up", 384, 400))
+        ts(R("bk"), R("bi"), 1023, A.bitwise_and)
+        tt(R("bk2"), R("bk"), R(lv), A.subtract)
         mm(R("dp0", 256, 512), R("IDb"), R("rr"), True, False)
         mm(R("dp0", 256, 512), R("NIDb"), R(x), False, True)
         act(R("rx"), R("dp0", 256, 512), F.Copy)
@@ -551,28 +545,28 @@ def rank_program(g, core, T, topo):
         tt(R("winm"), R("ov", 256, 512), R("wm"), A.is_lt)
         for h in range(2):
             hs = (128 * h, 128 * h + 128)
+            mm(R("up", 320 + 8 * h, 328 + 8 * h), R("wm", *hs), R("G8"))
+            mm(R("up", 336 + 8 * h, 344 + 8 * h), R("dpm", *hs), R("G8f"))
+        for h in range(2):
+            mm(R("up", 352 + 8 * h, 360 + 8 * h), R("winm", 128 * h, 128 * h + 128), R("G8"))
+        for h in range(2):
+            hs = (128 * h, 128 * h + 128)
             mm(R("dp1", *hs), R("winb", *hs), R("IDb"))
+        mm(R("m0", 0, 256), R("cI" + st), R("pm"), True, False)
+        mm(R("m0", 0, 256), R("IDb"), R("pmI"), False, False)
         for h in range(2):
             hs = (128 * h, 128 * h + 128)
-            mm(R("up", 128 + 8 * h, 136 + 8 * h), R("wm", *hs), R("G8"))
-            mm(R("up", 144 + 8 * h, 152 + 8 * h), R("winm", *hs), R("G8"))
-            mm(R("up", 160 + 8 * h, 168 + 8 * h), R("dpm", *hs), R("G8f"))
-        for h in range(2):
-            hs = (128 * h, 128 * h + 128)
-            mm(R("m0", *hs), R("r2", *hs), R("IDf"), True, False)
-            mm(R("m0", *hs), R("pS", *hs), R("I4K"), False, True)
+            mm(R("m0", *hs), R("r2", *hs), R("IDf"), False, False)
+            mm(R("m0", *hs), R("pS", *hs), R("I4K"), False, h == 1)
         for h in range(2):
             hs = (128 * h, 128 * h + 128)
             mm(R("m1", *hs), R("NE", *hs), R("IDf"))
         act(R("NEs"), R("m1", 0, 256), F.Copy)
         tt(R("dp0", 0, 256), R("rx"), R("dp1", 0, 256), A.mult)
         tt(R(xn), R("dp0", 0, 256), R(x), A.add)
-        for m in range(16):
-            mm(R("m1", 256, 272), R("W1", 128 * m, 128 * m + 128), R(xn, m, 256, 16), m == 0, m == 15)
-        tt(R("newc"), R("m0", 0, 256), R(CA), A.add)
-        cp(R("ws"), R("up", 128, 160))
+        act(R("newc"), R("m0", 0, 256), F.Identity, 4095.0)
         tt(R("vt"), R(lv), R("trash"), A.subtract)
-        tt(R("of"), R("ws", 16, 32), R("vt"), A.mult)
+        tt(R("of"), R("vt"), R("up", 352, 368), A.mult)
         tt(R("of"), R("of"), R("trash"), A.add)
         cp(R("ofu"), R("of"))
         cp(P("ind", R("ET", 0, 2944), R("ofu")), R("newc"))
@@ -580,19 +574,15 @@ def rank_program(g, core, T, topo):
         tt(R("XT", n0, n0 + 256), R(x), R("dp1", 0, 256), A.mult)
         tt(R("NEw"), R("NEs"), R("dp1", 0, 256), A.mult)
         act(R("ET", n0, n0 + 256), R("NEw"), F.Identity, 4095.0)
-        cp(R("dn"), R("up", 160, 176))
+        cp(R("dn"), R("up", 336, 352))
         ts(R("dn"), R("dn"), 4095, A.bitwise_and)
         tt(R("b1"), R(lv), R("dn"), A.subtract)
-        tt(R("b1"), R("b1"), R("ws", 0, 16), A.mult)
+        tt(R("b1"), R("b1"), R("up", 320, 336), A.mult)
         tt(R("b1"), R("b1"), R("dn"), A.add)
-        cp(R("bi"), R("m1", 256, 272))
-        ts(R("bk"), R("bi"), 1023, A.bitwise_and)
-        tt(R("b2"), R("bk"), R(lv), A.subtract)
-        tt(R("b2"), R("b2"), R("ws", 16, 32), A.mult)
+        tt(R("b2"), R("bk2"), R("up", 352, 368), A.mult)
         tt(R(lvn), R("b1"), R("b2"), A.add)
         if not last:
             cp(R("lvu"), R(lvn))
-            tt(R(CAn), R(CA), R("pm256"), A.add)
         else:
             dma("y", T.ykids[:], T.ET[:, 0:W], [R("ET", 0, W)], [])
             dma("s", T.ycand[:], T[xn][:], [R(xn)], [])

from concourse.mybir import dt, AluOpType as A, ActivationFunctionType as F

M, L, STEPS, H = 1792, 256, 3, 4096
W = M + L * STEPS
NENG = 8
BIG = float(2 ** 23)

SB = {
    "XT": (4096, "bfloat16"), "BK": (4096, "bfloat16"), "ET": (2944, "float32"), "KI": (M, "int32"), "IDX": (2304, "float32"),
    "ONE": (1024, "bfloat16"), "ZER": (128, "bfloat16"), "IDb": (128, "bfloat16"), "NIDb": (128, "bfloat16"), "IDf": (128, "float32"), "NIDf": (128, "float32"),
    "N20": (128, "bfloat16"), "N22": (128, "bfloat16"), "I4K": (128, "bfloat16"), "G8t": (8, "bfloat16"), "G8": (8, "bfloat16"), "G8f": (8, "float32"),
    "GW": (16, "float32"), "W1": (2048, "bfloat16"), "W2": (2048, "bfloat16"), "GS": (24, "bfloat16"), "GO": (8, "bfloat16"), "GO2": (8, "bfloat16"),
    "PICK": (1024, "bfloat16"), "PK8": (8, "bfloat16"), "TRI": (128, "bfloat16"), "pms": (128, "bfloat16"), "pm": (256, "bfloat16"), "npm": (256, "bfloat16"),
    "pmn": (256, "float32"), "rmf": (128, "float32"), "rmb": (128, "bfloat16"), "CR": (512, "bfloat16"), "REP": (2048, "bfloat16"), "trash": (16, "float32"),
    "II": (256, "bfloat16"), "pmI": (256, "bfloat16"), "cI0": (128, "bfloat16"), "cI1": (128, "bfloat16"), "cI2": (128, "bfloat16"),
    "wt": (2, "bfloat16"), "sp": (16, "int32"), "x0": (256, "bfloat16"), "x1": (256, "bfloat16"), "lv0": (16, "float32"), "lv1": (16, "float32"), "lvu": (16, "uint16"),
    "Ei": (256, "int32"), "Ci": (256, "int32"), "CL": (256, "uint16"), "Ff": (256, "float32"), "em": (256, "bfloat16"), "Cm": (256, "float16"), "Rm": (256, "float32"),
    "vA": (256, "float16"), "vcol": (16, "float32"), "xT": (256, "bfloat16"), "d0": (256, "bfloat16"),
    "XG": (4096, "bfloat16"), "DD": (4096, "bfloat16"), "SG": (4096, "bfloat16"), "CMP": (4096, "bfloat16"), "HL": (256, "uint16"),
    "hu0": (256, "int32"), "hp0": (128, "int32"), "hu1": (256, "int32"), "hp1": (128, "int32"), "ru": (32, "int32"), "rp": (16, "int32"), "rl": (16, "uint16"), "MQ": (3072, "bfloat16"), "MD": (3072, "bfloat16"),
    "tA": (256, "float32"), "cap": (256, "bfloat16"), "nc": (256, "bfloat16"), "key": (256, "float32"), "wm": (256, "bfloat16"), "w1s": (256, "bfloat16"), "wb": (256, "bfloat16"),
    "k1": (256, "float32"), "k2": (256, "float32"), "dpm": (256, "float32"), "NE": (256, "float32"), "n1": (256, "float32"), "n2": (256, "float32"), "Si": (256, "int32"), "pS": (256, "bfloat16"),
    "r2": (256, "float32"), "winb": (256, "bfloat16"), "winm": (256, "bfloat16"), "newc": (256, "float32"), "NEs": (256, "float32"), "NEw": (256, "float32"),
    "rr": (256, "bfloat16"), "rx": (256, "bfloat16"), "ws": (32, "float32"), "of": (16, "float32"), "ofu": (16, "uint16"), "vt": (16, "float32"),
    "dn": (16, "int32"), "bk2": (16, "float32"), "b1": (16, "float32"), "b2": (16, "float32"), "bi": (16, "int32"), "bk": (16, "int32"),
}
for _t in range(STEPS):
    for _n in ("z", "zl", "yr", "yl"):
        SB[_n + str(_t)] = (256, "bfloat16")
PS = ["dp0", "dp1", "up", "BH0", "BH1", "ov", "m0", "m1"]
SCRATCH = {k: ("sbuf", [128, n], d) for k, (n, d) in SB.items()}
for _n in PS:
    SCRATCH[_n] = ("psum", [128, 512], "float32")
NDMA = 10
SEMAPHORES = ["qv", "qs", "qt", "qg"] + ["D%d" % i for i in range(NDMA)] + [n + str(t) for t in range(STEPS) for n in ("zs", "za", "ys", "ya")]


ORDER = {}
CYC = 0.83e-3
PECYC = 0.45e-3
WAKE = 0.18
CHUNKS = ((0, 2), (2, 4), (4, 6), (6, 8))
G1V = ()
SGV = (0,)
MQV = tuple(range(8))


def overlap(a, b):
    return a[1] < b[2] and b[1] < a[2] and not (a[3] == b[3] and a[3] > 1 and (a[1] - b[1]) % a[3])


def schedule(nodes, psum):
    wake = WAKE
    n = len(nodes)
    preds = [[] for _ in range(n)]
    hist = {}
    for i in range(n):
        kind, q, fn, reads, writes, cost, sem = nodes[i]
        seen = {}
        for rs, w in ((reads, False), (writes, True)):
            for r in rs:
                bank = r[0] in psum
                for (j, rj, wj) in hist.get(r[0], ()):
                    ov = overlap(r, rj)
                    same = nodes[j][1] == q and kind == "c" and nodes[j][0] == "c"
                    if bank and (q == "t" or not same):
                        full = not same or (ov and wj and q != "t")
                    elif ov and (w or wj):
                        full = not same or wj
                    else:
                        continue
                    seen[j] = seen.get(j, False) or full
        preds[i] = list(seen.items())
        for rs, w in ((reads, False), (writes, True)):
            for r in rs:
                h = hist.get(r[0], [])
                if w and abs(r[3]) == 1 and r[4] == 128 and r[0] not in psum:
                    h = [e for e in h if not (r[1] <= e[1][1] and e[1][2] <= r[2])]
                if r[0] in psum and len(h) > 40:
                    h = h[-40:]
                hist[r[0]] = h + [(i, r, w)]
    succ = [[] for _ in range(n)]
    for i in range(n):
        for j, full in preds[i]:
            succ[j].append((i, full))
    prio = [0.0] * n
    for i in range(n - 1, -1, -1):
        c = nodes[i][5]
        prio[i] = max([c] + [prio[k] + (c + wake if full else 0.0) for k, full in succ[i]])
        if nodes[i][0] == "d":
            prio[i] += 1e7 - 1e3 * i
    left = [len(p) for p in preds]
    ready = {}
    free = {}
    est = [0.0] * n
    for i in range(n):
        if not left[i]:
            ready.setdefault(nodes[i][1], []).append(i)
    order = []
    while len(order) < n:
        best = None
        for q, r in ready.items():
            if r:
                t = min(max(est[i], free.get(q, 0.0)) for i in r)
                if best is None or t < best[0]:
                    best = (t, q)
        t, q = best
        i = max((k for k in ready[q] if max(est[k], free.get(q, 0.0)) <= t + 0.02), key=lambda k: (prio[k], -k))
        ready[q].remove(i)
        st = max(est[i], free.get(q, 0.0))
        end = st + nodes[i][5]
        free[q] = end if nodes[i][0] == "c" else st + (0.1 if nodes[i][0] == "d" else 1.0)
        order.append(i)
        for k, full in succ[i]:
            est[k] = max(est[k], end + wake if full else st)
            left[k] -= 1
            if not left[k]:
                ready.setdefault(nodes[k][1], []).append(k)
    return order


def rank_program(g, core, T, topo):
    rank = T.rank_of(core)
    if rank is None:
        return
    queues = {"v": g.vector, "s": g.scalar, "t": g.tensor, "g": g, "y": g.sync}
    known = {q: {} for q in queues}
    count = {}
    clock = {}
    hist = {}

    def R(name, lo=0, hi=None, step=1, p1=128):
        return (name, lo, SB[name][0] if hi is None and name in SB else (512 if hi is None else hi), step, p1)

    def P(name, win, off):
        return ("ind", win, off)

    def ap(r):
        if r[0] == "ind":
            return ap(r[1]).indirect(ap(r[2]))
        name, lo, hi, step, p1 = r
        if step == -1:
            return T[name][:, hi - 1:(lo - 1 if lo > 0 else None):-1]
        if p1 != 128:
            return T[name][0:p1, lo:hi]
        return T[name][:, lo:hi] if step == 1 else T[name][:, lo:hi:step]

    def flat(rs):
        out = []
        for r in rs:
            out += [r[1], r[2]] if r[0] == "ind" else [r]
        return out

    def need(q, ev):
        sem, val = ev
        k = known[q]
        if k.get(sem, 0) >= val:
            return
        queues[q].wait_ge(T.sem[sem], val)
        k[sem] = val
        for s2, v2 in clock.get(ev, {}).items():
            if k.get(s2, 0) < v2:
                k[s2] = v2

    def deps(q, me, reads, writes):
        evs = {}
        for rs, w in ((reads, False), (writes, True)):
            for r in rs:
                bank = r[0] in PS
                for (who, ev, lo, hi, wasw, step) in hist.get(r[0], ()):
                    over = lo < r[2] and r[1] < hi and not (step == r[3] and step > 1 and (lo - r[1]) % step)
                    if who == me:
                        if not wasw or not over or (w and me == "t"):
                            continue
                    elif not (bank or (over and (w or wasw))):
                        continue
                    if evs.get(ev[0], 0) < ev[1]:
                        evs[ev[0]] = ev[1]
        for sem in sorted(evs):
            need(q, (sem, evs[sem]))

    def note(me, ev, reads, writes):
        for rs, w in ((reads, False), (writes, True)):
            for r in rs:
                old = hist.get(r[0], [])
                if w and abs(r[3]) == 1 and r[4] == 128:
                    old = [e for e in old if not (r[1] <= e[2] and e[3] <= r[2])]
                else:
                    old = [e for e in old if not (e[0] == me and e[2:] == (r[1], r[2], w, abs(r[3])))]
                hist[r[0]] = old + [(me, ev, r[1], r[2], w, abs(r[3]))]

    nodes = []

    def emit(q, fn, reads, writes, cost):
        nodes.append(("c", q, fn, flat(reads), flat(writes), cost, None))

    nd = [0]

    def dma(q, out, in_, reads, writes):
        sem = "D%d" % nd[0]
        nd[0] += 1
        size = 128 * (writes or reads)[0][2] * 4
        nodes.append(("d", q, lambda: queues[q].dma_start(out, in_), reads, writes, 2.0 + size / 2.0e5, sem))

    def send(src, dst, peer, lsem, rsem):
        to = T.cores[peer]
        rid, pid = topo.addr(to)[:2]
        engs = topo.engines(core, to)[:NENG]

        def fn():
            g.remote_dma(T[dst][:], T[src][:], T.sem[rsem], T.sem[lsem], pid, rid, sum(1 << e for e in engs))
        nodes.append(("r", "g", fn, [R(src)], [R(dst)], 5.0, (lsem, len(engs))))

    def finish():
        order = ORDER.get("order")
        if order is None or len(order) != len(nodes):
            order = schedule(nodes, PS)
            ORDER["order"] = order
        for i in order:
            kind, q, fn, reads, writes, cost, sem = nodes[i]
            if kind == "c":
                deps(q, q, reads, writes)
                name = "q" + q
                count[name] = count.get(name, 0) + 1
                fn().then_inc(T.sem[name], 1)
                ev, me = (name, count[name]), q
            elif kind == "d":
                deps(q, sem, reads, writes)
                fn().then_inc(T.sem[sem], 16)
                count[sem] = 16
                ev, me = (sem, 16), sem
            else:
                deps("g", sem[0], reads, [])
                fn()
                count[sem[0]] = sem[1]
                ev, me, writes = sem, sem[0], []
            clock[ev] = dict(known[q])
            note(me, ev, reads, writes)
        for sem in sorted(count):
            need("g", (sem, count[sem]))

    for t in range(STEPS):
        for buf, sem in (("zl", "za"), ("yl", "ya")):
            hist[buf + str(t)] = [("remote", (sem + str(t), NENG), 0, 256, True, 1)]
            count[sem + str(t)] = NENG

    def width(r):
        return 16 * width(r[2]) if r[0] == "ind" else -((r[1] - r[2]) // abs(r[3]))

    def dtype_of(r):
        return "float32" if r[0] in PS else SB[r[0]][1]

    def vcost(out, ins, kind):
        if out[0] == "ind":
            return 0.05 + 4.0 * width(out[2]) * 16 * CYC
        n = width(out)
        if any(r[0] == "ind" for r in ins):
            return 0.05 + 1.56 * n * CYC
        if kind == 2:
            c = n if any(r[0] in PS for r in ins) else 2 * n
        else:
            c = n
            if kind == 1 and all(dtype_of(r) not in ("float32", "int32") for r in [out] + ins if width(r) > 1):
                c = n / 2
        return max(64, c) * CYC

    V, S, TE = g.vector, g.scalar, g.tensor

    def tt(out, a, b, op):
        emit("v", lambda: V.tensor_tensor(ap(out), ap(a), ap(b), op), [a, b], [out], vcost(out, [a, b], 2))

    def ts(out, a, s1, op0, s2=None, op1=None):
        rs = [a] + [s for s in (s1, s2) if not isinstance(s, (int, float)) and s is not None]
        c1 = s1 if isinstance(s1, (int, float)) else ap(s1)
        if op1 is None:
            emit("v", lambda: V.tensor_scalar(ap(out), ap(a), c1, None, op0), rs, [out], vcost(out, [a], 1))
        else:
            c2 = s2 if isinstance(s2, (int, float)) else ap(s2)
            emit("v", lambda: V.tensor_scalar(ap(out), ap(a), c1, c2, op0, op1), rs, [out], vcost(out, [a], 1))

    def cp(out, a):
        emit("v", lambda: V.tensor_copy(ap(out), ap(a)), [a], [out], vcost(out, [a], 1))

    def fill(out, c):
        emit("v", lambda: V.memset(ap(out), c), [], [out], vcost(out, [], 1))

    def scan(out, d0, d1):
        emit("v", lambda: V.tensor_tensor_scan(ap(out), ap(d0), ap(d1), 0.0, A.mult, A.max), [d0, d1], [out], vcost(out, [d0, d1], 1))

    def act(out, a, f, bias=0.0, scale=1.0):
        col = not isinstance(bias, (int, float))
        emit("s", lambda: S.activation(ap(out), ap(a), f, bias=ap(bias) if col else bias, scale=scale), [a] + ([bias] if col else []), [out], vcost(out, [a], 0))

    def mm(out, lhsT, rhs, start=True, stop=True):
        cost = max(64, width(rhs)) * (4 if dtype_of(lhsT) == "float32" else 1) * PECYC
        emit("t", lambda: TE.matmul(ap(out), ap(lhsT), ap(rhs), start, stop), [lhsT, rhs], [out], cost)

    def aff(out, a, pat, op, fl, base, cm):
        emit("g", lambda: g.affine_select(ap(out), ap(a), pat, op, fl, base, cm), [a], [out], 0.17 + 2 * width(out) * CYC)

    def iota(out, pat, base, cm):
        emit("g", lambda: g.iota(ap(out), pat, base, cm, allow_small_or_imprecise_dtypes=True), [], [out], 0.13 + 2 * width(out) * CYC)

    dma("y", T.sp[:], T.spot[:], [], [R("sp")])
    dma("y", T.KI[:], T.kids[:], [], [R("KI")])
    dma("s", T.wt[:], T.wts[:], [], [R("wt")])
    dma("s", T.x0[:], T.cand[:], [], [R("x0")])
    dma("s", T.XT[:, 0:M], T.nodes[:], [], [R("XT", 0, M)])
    dma("y", T.BK[:], T.book[:], [], [R("BK")])

    fill(R("ONE"), 1.0)
    fill(R("ZER"), 0.0)
    aff(R("IDb"), R("ONE", 0, 128), [[-1, 128]], A.is_equal, 0.0, 0, 1)
    aff(R("G8t"), R("ONE", 0, 8), [[-16, 8]], A.is_ge, 0.0, 0, 1)
    aff(R("G8"), R("G8t"), [[16, 8]], A.is_ge, 0.0, 15, -1)
    fill(R("W1"), 0.0)
    fill(R("W2"), 0.0)
    fill(R("XT", M, 4096), 0.0)
    ts(R("NIDb"), R("IDb"), -1.0, A.mult)
    for m in range(16):
        cp(R("REP", m, 2048, 16), R("IDb"))
    cp(R("G8f"), R("G8"))
    cp(R("lvu"), R("sp"))
    cp(R("lv0"), R("sp"))
    for j, w in ((0, "W1"), (1, "W2")):
        ts(R("GW", 8 * j, 8 * j + 8), R("G8f"), R("wt", j, j + 1), A.mult)
        for q in range(8):
            ts(R(w, 16 * q, 16 * q + 129 * 15 + 1, 129), R("ONE", 0, 16), R("GW", 8 * j + q, 8 * j + q + 1), A.mult)
    aff(R("PK8"), R("ONE", 0, 8), [[-16, 8]], A.is_equal, 0.0, 0, 1)
    aff(R("TRI"), R("ZER"), [[1, 128]], A.is_gt, -8192.0, 0, -1)
    iota(R("IDX"), [[1, 2304]], -1280, 0)
    fill(R("CR"), 0.0)
    fill(R("CR", 128, 256, 1, 2), 2048.0)
    fill(R("CR", 256, 384, 1, 2), 1.0)
    fill(R("CR", 256, 384, 1, 1), -2048.0)
    iota(R("CR", 128, 256, 1, 1), [[0, 8], [-4096, 16]], 65536, 0)
    iota(R("II"), [[1, 256]], 1, 0)
    fill(R("CR", 0, 128, 1, 2), 1.0)
    fill(R("CR", 0, 128, 1, 1), -4096.0)
    iota(R("trash"), [[16, 16]], W, 1)

    def more_constants():
        cp(R("IDf"), R("IDb"))
        ts(R("NIDf"), R("IDb"), -1.0, A.mult)
        ts(R("N20"), R("IDb"), -float(2 ** 20), A.mult)
        ts(R("N22"), R("IDb"), -float(2 ** 22), A.mult)
        ts(R("I4K"), R("IDb"), 4096.0, A.mult)
        for z, c in ((0, 4096.0), (8, 65536.0), (16, 4096.0)):
            ts(R("GS", z, z + 8), R("G8"), c, A.mult)
        ts(R("GO"), R("G8"), -float(2 ** 19), A.mult)
        if SGV:
            ts(R("GO2"), R("G8"), -float(2 ** 20), A.mult)
        tt(R("pms", 0, 64), R("IDb", 0, 64), R("IDb", 64, 128), A.add)
        tt(R("pms", 64, 96), R("pms", 0, 32), R("pms", 32, 64), A.add)
        tt(R("pm", 0, 16), R("pms", 64, 80), R("pms", 80, 96), A.add)
        for n in (16, 32, 64, 128):
            cp(R("pm", n, 2 * n), R("pm", 0, n))
        ts(R("npm"), R("pm"), -1.0, A.mult, 1.0, A.add)

    def even_more():
        ts(R("pmn"), R("pm"), BIG + 1.0, A.mult, -BIG, A.add)
        fill(R("rmf"), 1.0)
        fill(R("rmb"), 1.0)
        ts(R("rmf", 0, 128, 16), R("ONE", 0, 8), 0.0, A.mult)
        ts(R("rmb", 0, 128, 16), R("ONE", 0, 8), 0.0, A.mult)
        tt(R("pmI"), R("pm"), R("II"), A.mult)
        for u in range(STEPS):
            ts(R("cI%d" % u), R("IDb"), -2304.0 + 256.0 * u, A.mult)
        cp(R("ET", 0, M), R("KI"))
        fill(R("ET", M, W), 4095.0)

    def hash_ops(u, n, ui, p, out):
        cp(R(ui, 0, 2 * n), u)
        ts(R(ui, 0, 2 * n), R(ui, 0, 2 * n), 4095, A.bitwise_and)
        tt(R(p, 0, n), R(ui, 0, n), R(ui, n, 2 * n), A.mult)
        ts(R(p, 0, n), R(p, 0, n), 5, A.arith_shift_right)
        tt(R(p, 0, n), R(p, 0, n), R(ui, n, 2 * n), A.add)
        ts(R(p, 0, n), R(p, 0, n), 4095, A.bitwise_and)
        cp(out, R(p, 0, n))

    for t in range(STEPS):
        x, xn = ("x0", "x1") if t % 2 == 0 else ("x1", "x0")
        lv, lvn = ("lv0", "lv1") if t % 2 == 0 else ("lv1", "lv0")
        st = str(t)
        last = t == STEPS - 1
        tab = ("KI", M) if t == 0 else ("ET", M + 256 * (t - 1))

        def G1(b0, b1):
            if b0 in G1V:
                cp(R("XG", 512 * b0, 512 * b1), P("ind", R("XT"), R("CL", 32 * b0, 32 * b1)))
            else:
                act(R("XG", 512 * b0, 512 * b1), P("ind", R("XT"), R("CL", 32 * b0, 32 * b1)), F.Copy)

        def sub(j):
            h, b = j // 4, "dp%d" % (j % 2)
            mm(R(b), R("NIDb"), R("XG", 512 * j, 512 * j + 512), True, False)
            mm(R(b), R("xT", 128 * h, 128 * h + 128), R("REP", 512 * (j % 4), 512 * (j % 4) + 512), False, True)
            act(R("DD", 512 * j, 512 * j + 512), R(b), F.Abs)
            if h in SGV:
                ts(R("SG", 512 * j, 512 * j + 512), R(b), 0.0, A.is_ge)
            else:
                act(R("SG", 512 * j, 512 * j + 512), R(b), F.Sign, 0.5)

        def hashes(b0, b1, c):
            n = 32 * (b1 - b0)
            for u, w in ((0, "W1"), (n, "W2")):
                for k in range(16):
                    mm(R("up", u, u + n), R(w, 128 * k, 128 * k + 128), R("DD", 512 * b0 + k, 512 * b1, 16), k == 0, k == 15)
            hash_ops(R("up", 0, 2 * n), n, "hu%d" % (c % 2), "hp%d" % (c % 2), R("HL", 32 * b0, 32 * b1))
            tt(R("CMP", 512 * b0, 512 * b1), P("ind", R("BK"), R("HL", 32 * b0, 32 * b1)), R("DD", 512 * b0, 512 * b1), A.is_ge)

        def over(h):
            for k in range(16):
                mm(R("ov", 128 * h + k, 128 * h + 128, 16), R("SG", 2048 * h + k, 2048 * h + 2048, 16), R("GO2" if h in SGV else "GO"))
            act(R("tA", 128 * h, 128 * h + 128), R("ov", 128 * h, 128 * h + 128), F.Relu, 11.5 * 2 ** 20 - (0.0 if h in SGV else BIG) - 4095.0)

        def scount(h):
            for k in range(16):
                mm(R("BH%d" % h, k, 384, 16), R("CMP", 2048 * h + k, 2048 * h + 2048, 16), R("GS"), False, k == 15)

        def bh_open(h):
            b = "BH%d" % h
            hs = (128 * h, 128 * h + 128)
            mm(R(b), R("ONE", 0, 128), R("CR"), True, False)
            mm(R(b, 0, 128), R("Ff", *hs), R("NIDf"), False, False)
            mm(R(b, 0, 128), R("em", *hs), R("N20"), False, False)
            mm(R(b, 128, 256), R("Cm", *hs), R("IDb"), False, False)
            mm(R(b, 128, 256), R("em", *hs), R("N22"), False, False)
            mm(R(b, 256, 384), R("Cm", *hs), R("IDb"), False, False)
            mm(R(b, 384, 512), R("Rm", *hs), R("IDf"), False, False)

        def same(q):
            b = "m%d" % (q % 2)
            pk = R("PICK", 128 * q, 128 * q + 128)
            mm(R(b, 0, 128), R("IDb"), R("TRI"), True, False)
            mm(R(b, 0, 128), pk, R("vA", 0, 128), False, True)
            mm(R(b, 128, 256), pk, R("vA", 128, 256))
            mm(R(b, 256, 384), R("IDb"), R("TRI"), True, False)
            mm(R(b, 256, 384), pk, R("vA", 128, 256), False, True)
            o = 384 * q
            if q in MQV:
                ts(R("MQ", o, o + 256), R(b, 0, 256), R("vcol", q, q + 1), A.add, 0.0, A.is_equal)
                ts(R("MQ", o + 256, o + 384), R(b, 256, 384), R("vcol", 8 + q, 9 + q), A.add, 0.0, A.is_equal)
                return
            act(R("MD", o, o + 256), R(b, 0, 256), F.Abs, R("vcol", q, q + 1))
            act(R("MD", o + 256, o + 384), R(b, 256, 384), F.Abs, R("vcol", 8 + q, 9 + q))
            if q % 2:
                ts(R("MQ", o - 384, o + 384), R("MD", o - 384, o + 384), 0.0, A.is_equal)

        def decide(h):
            b = "BH%d" % h
            lo, hi = 128 * h, 128 * h + 128

            def r(n, step=1):
                return R(n, lo, hi, step)
            tt(r("cap"), R(b, 0, 128), r("tA"), A.is_gt)
            tt(r("nc"), R(b, 0, 128), r("tA"), A.is_le)
            tt(R(b, 128, 256), r("nc"), R(b, 128, 256), A.mult)
            tt(r("wm"), r("pmn"), R(b, 128, 256), A.is_gt)
            scan(r("w1s"), R("rmb"), r("wm"))
            scan(r("wb", -1), R("rmb"), r("w1s", -1))

        def decide2(h):
            b = "BH%d" % h
            lo, hi = 128 * h, 128 * h + 128

            def r(n, step=1):
                return R(n, lo, hi, step)
            tt(r("r2"), r("nc"), R(b, 384, 512), A.mult)
            tt(r("NE"), r("cap"), R(b, 256, 384), A.mult)
            scan(r("n1"), R("rmf"), r("NE"))
            scan(r("n2", -1), R("rmf"), r("n1", -1))
            ts(r("Si"), r("n2"), 2.0 ** -12, A.mult, 0.5 - 2.0 ** -13, A.add)
            tt(r("pS"), r("Si"), r("pm"), A.mult)
            scan(r("k1"), R("rmf"), R(b, 128, 256))
            scan(R(b, 128, 256, -1), R("rmf"), r("k1", -1))
            tt(r("dpm"), r("pm"), R(b, 128, 256), A.mult)

        for a, b in ((0, 64), (64, 256)):
            cp(R("Ei", a, b), P("ind", R(tab[0], 0, tab[1]), R("lvu", a // 16, b // 16)))
            ts(R("Ci", a, b), R("Ei", a, b), 4095, A.bitwise_and)
            cp(R("CL", a, b), R("Ci", a, b))
        tt(R("d0"), P("ind", R("XT"), R("lvu")), R(x), A.subtract)
        for h in range(2):
            mm(R("m0", 128 * h, 128 * h + 128), R(x, 128 * h, 128 * h + 128), R("IDb"))
        act(R("xT"), R("m0", 0, 256), F.Copy)
        act(R("z" + st), R("d0"), F.Abs)
        send("z" + st, "zl" + st, (rank + 1 + t) % 4, "zs" + st, "za" + st)
        for b0, b1 in CHUNKS:
            G1(b0, b1)
        if t == 0:
            aff(R("PICK"), R("ONE"), [[-16, 8], [0, 128]], A.is_equal, 0.0, 0, 1)
            more_constants()
        ts(R("Ff"), R("Ei"), -4095.0, A.add)
        ts(R("em"), R("Ci"), 4095.0, A.is_equal)
        ts(R("Cm"), R("Ci"), -2048.0, A.add)
        tt(R("Rm"), R("Ff"), R("npm"), A.mult)
        cp(R("vA"), P("ind", R("IDX"), R("lvu")))
        for h in range(2):
            mm(R("m1", 8 * h, 8 * h + 8), R("vA", 128 * h, 128 * h + 128), R("PK8"))
        ts(R("vcol"), R("m1", 0, 16), -1.0, A.mult)
        bh_open(0)
        bh_open(1)
        if t == 0:
            even_more()
        for c, (b0, b1) in enumerate(CHUNKS):
            for j in range(b0, b1):
                sub(j)
                if j in (3, 7):
                    over(j // 4)
                if j == 3:
                    for u, w in ((256, "W1"), (272, "W2")):
                        for m in range(16):
                            mm(R("ov", u, u + 16), R(w, 128 * m, 128 * m + 128), R("zl" + st, m, 256, 16), m == 0, m == 15)
                    hash_ops(R("ov", 256, 288), 16, "ru", "rp", R("rl"))
                    act(R("yr" + st), P("ind", R("BK"), R("rl")), F.Copy)
                    send("yr" + st, "yl" + st, (rank - 1 - t) % 4, "ys" + st, "ya" + st)
            hashes(b0, b1, c)
            if b1 in (4, 8):
                scount(b1 // 4 - 1)
        for q in range(8):
            same(q)
        decide(0)
        decide2(0)
        mm(R("dp0", 0, 256), R("IDb"), R("yl" + st), True, False)
        mm(R("dp0", 0, 256), R("NIDb"), R(x), False, True)
        act(R("rr"), R("dp0", 0, 256), F.Abs)
        for m in range(16):
            mm(R("up", 384, 400), R("W1", 128 * m, 128 * m + 128), R("rr", m, 256, 16), m == 0, m == 15)
        cp(R("bi"), R("up", 384, 400))
        ts(R("bk"), R("bi"), 1023, A.bitwise_and)
        tt(R("bk2"), R("bk"), R(lv), A.subtract)
        mm(R("dp0", 256, 512), R("IDb"), R("rr"), True, False)
        mm(R("dp0", 256, 512), R("NIDb"), R(x), False, True)
        act(R("rx"), R("dp0", 256, 512), F.Copy)
        decide(1)
        for hi in range(2):
            for q in range(8):
                o = 256 + 128 * hi + 16 * q
                mm(R("ov", o, o + 16), R("MQ", 384 * q + 128 * hi, 384 * q + 128 * hi + 128), R("wb", 16 * q, 16 * q + 16), True, hi == 0)
                if hi == 1:
                    mm(R("ov", o, o + 16), R("MQ", 384 * q + 256, 384 * q + 384), R("wb", 128 + 16 * q, 144 + 16 * q), False, True)
        decide2(1)
        tt(R("winb"), R("ov", 256, 512), R("wb"), A.is_lt)
        tt(R("winm"), R("ov", 256, 512), R("wm"), A.is_lt)
        for h in range(2):
            hs = (128 * h, 128 * h + 128)
            mm(R("up", 320 + 8 * h, 328 + 8 * h), R("wm", *hs), R("G8"))
            mm(R("up", 336 + 8 * h, 344 + 8 * h), R("dpm", *hs), R("G8f"))
        for h in range(2):
            mm(R("up", 352 + 8 * h, 360 + 8 * h), R("winm", 128 * h, 128 * h + 128), R("G8"))
        for h in range(2):
            hs = (128 * h, 128 * h + 128)
            mm(R("dp1", *hs), R("winb", *hs), R("IDb"))
        mm(R("m0", 0, 256), R("cI" + st), R("pm"), True, False)
        mm(R("m0", 0, 256), R("IDb"), R("pmI"), False, False)
        for h in range(2):
            hs = (128 * h, 128 * h + 128)
            mm(R("m0", *hs), R("r2", *hs), R("IDf"), False, False)
            mm(R("m0", *hs), R("pS", *hs), R("I4K"), False, h == 1)
        for h in range(2):
            hs = (128 * h, 128 * h + 128)
            mm(R("m1", *hs), R("NE", *hs), R("IDf"))
        act(R("NEs"), R("m1", 0, 256), F.Copy)
        tt(R("dp0", 0, 256), R("rx"), R("dp1", 0, 256), A.mult)
        tt(R(xn), R("dp0", 0, 256), R(x), A.add)
        act(R("newc"), R("m0", 0, 256), F.Identity, 4095.0)
        tt(R("vt"), R(lv), R("trash"), A.subtract)
        tt(R("of"), R("vt"), R("up", 352, 368), A.mult)
        tt(R("of"), R("of"), R("trash"), A.add)
        cp(R("ofu"), R("of"))
        cp(P("ind", R("ET", 0, 2944), R("ofu")), R("newc"))
        n0 = M + 256 * t
        tt(R("XT", n0, n0 + 256), R(x), R("dp1", 0, 256), A.mult)
        tt(R("NEw"), R("NEs"), R("dp1", 0, 256), A.mult)
        act(R("ET", n0, n0 + 256), R("NEw"), F.Identity, 4095.0)
        cp(R("dn"), R("up", 336, 352))
        ts(R("dn"), R("dn"), 4095, A.bitwise_and)
        tt(R("b1"), R(lv), R("dn"), A.subtract)
        tt(R("b1"), R("b1"), R("up", 320, 336), A.mult)
        tt(R("b1"), R("b1"), R("dn"), A.add)
        tt(R("b2"), R("bk2"), R("up", 352, 368), A.mult)
        tt(R(lvn), R("b1"), R("b2"), A.add)
        if not last:
            cp(R("lvu"), R(lvn))
        else:
            dma("y", T.ykids[:], T.ET[:, 0:W], [R("ET", 0, W)], [])
            dma("s", T.ycand[:], T[xn][:], [R(xn)], [])
            dma("s", T.ynodes[:], T.XT[:, M:W], [R("XT", M, W)], [])
            dma("s", T.yspot[:], T[lvn][:], [R(lvn)], [])

    finish()
